import numpy as np
import ml_dtypes


def mxq(x, axis, fmt="e4m3"):
    dtype, down = {"e4m3": (ml_dtypes.float8_e4m3fn, 7), "e5m2": (ml_dtypes.float8_e5m2, 14)}[fmt]
    v = np.moveaxis(np.asarray(x, np.float32).astype(ml_dtypes.bfloat16).astype(np.float64), axis, -1)
    blocks = v.reshape(v.shape[:-1] + (-1, 32))
    amax = np.abs(blocks).max(-1, keepdims=True)
    byte = np.maximum(np.where(amax > 0, np.frexp(amax)[1] - 1 + 127, 0) - down, 1)
    scale = np.exp2(byte - 127.0)
    codes = (blocks / scale).astype(np.float32).astype(dtype).astype(np.float64)
    return np.moveaxis((codes * scale).reshape(v.shape), -1, axis)


WIDE = False


def mx_kscale(k):
    if not WIDE:
        return np.ones(k)
    levels = np.array([10, -10, 5, -5, 0])
    if k % 512:
        return np.exp2(np.random.permutation(np.resize(levels, k // 32))).repeat(32)
    a = np.empty((k // 512, 16))
    for p in range(k // 512):
        a[p, :8] = np.random.permutation(np.resize(levels, 8))
        for g in range(8):
            far = levels[np.abs(levels - a[p, g]) >= 10]
            a[p, g + 8] = far[np.random.randint(len(far))]
    return np.exp2(a.ravel()).repeat(32)


BF16 = ml_dtypes.bfloat16


def bf(x):
    return np.asarray(x, np.float32).astype(BF16)


def f64(x):
    return np.asarray(x).astype(np.float64)


E2M1 = np.array([0.0, 0.5, 1.0, 1.5, 2.0, 3.0, 4.0, 6.0, -0.0, -0.5, -1.0, -1.5, -2.0, -3.0, -4.0, -6.0])


def pack_weight(w, fmt):
    k, n = w.shape
    w = f64(bf(w)).reshape(k // 32, 32, n)
    amax = np.abs(w).max(1)
    if fmt == "e4m3":
        byte = np.frexp(amax)[1] - 1 + 127 - 7
    else:
        mant, ex = np.frexp(amax / 6.0)
        byte = np.where(mant > 0.5, ex, ex - 1) + 127
    byte = np.clip(np.where(amax > 0, byte, 1), 1, 254)
    scaled = (w * np.exp2(127.0 - byte)[:, None, :]).reshape(k, n).astype(np.float32)
    by_word = np.ascontiguousarray(scaled.reshape(k // 512, 128, 4, n).transpose(0, 1, 3, 2))
    if fmt == "e4m3":
        words = by_word.astype(ml_dtypes.float8_e4m3fn).view(np.uint8)
    else:
        c = by_word.astype(ml_dtypes.float4_e2m1fn).view(np.uint8) & 0xF
        words = c[..., 0::2] | (c[..., 1::2] << 4)
    return np.ascontiguousarray(words), np.ascontiguousarray(byte.astype(np.uint8).reshape(k // 512, 16, n))


def unpack_weight(words, scales, fmt):
    g, p, n, _ = words.shape
    if fmt == "e4m3":
        vals = np.ascontiguousarray(words).view(ml_dtypes.float8_e4m3fn).astype(np.float64)
    else:
        nib = np.empty((g, p, n, 4), np.uint8)
        nib[..., 0::2] = words & 0xF
        nib[..., 1::2] = words >> 4
        vals = E2M1[nib]
    vals = vals * np.repeat(np.exp2(scales.astype(np.float64) - 127.0), 8, axis=1)[..., None]
    return vals.transpose(0, 1, 3, 2).reshape(g * 512, n)
def pack4(w):
    words, scales = pack_weight(w, "e2m1")
    return words.reshape(words.shape[0], 128, -1), scales


def unpack4(words, scales):
    return unpack_weight(words.reshape(words.shape[0], 128, -1, 2), scales, "e2m1")


def planes(Y):
    n, m = Y.shape
    b = f64(bf(Y)).reshape(n // 32, 32, m)
    amax = np.abs(b).max(1)
    byte = np.clip(np.where(amax > 0, np.frexp(amax)[1] - 1 + 127 - 7, 1), 1, 254)
    codes = (b * np.exp2(127.0 - byte)[:, None, :]).reshape(n, m).astype(np.float32).astype(ml_dtypes.float8_e4m3fn).view(np.uint8)
    words = codes.reshape(n // 512, 128, 4, m).transpose(0, 1, 3, 2)
    return np.ascontiguousarray(words), np.ascontiguousarray(byte.astype(np.uint8).reshape(n // 512, 16, m))


H, T, D, S, E = 4, 512, 512, 1024, 1024


def setup_inputs():
    s = mx_kscale(D)
    t = mx_kscale(H * S)
    spread = np.exp(0.8 * np.random.randn(E))
    queries = bf(np.random.randn(H, T, D) * s)
    kt_words, kt_scales = pack4(1.5 * np.random.randn(D, S) / np.sqrt(D) / s[:, None])
    score_bias = bf(0.5 * np.random.randn(H, S) - 1.0)
    key_gain = bf((1.0 + 0.1 * np.random.randn(H, S)) * t.reshape(H, S))
    vo_words, vo_scales = pack4(2.0 * np.random.randn(H * S, E) / np.sqrt(H * S) / t[:, None])
    out_bias = bf(0.3 * np.random.randn(E))
    layer_scale = bf(spread)
    x = bf(0.7 * np.random.randn(T, E) * spread)
    return {"queries": queries, "kt_words": kt_words, "kt_scales": kt_scales,
            "score_bias": score_bias, "key_gain": key_gain,
            "vo_words": vo_words, "vo_scales": vo_scales,
            "out_bias": out_bias, "layer_scale": layer_scale, "x": x}

def reference(queries, kt_words, kt_scales, score_bias, key_gain, vo_words, vo_scales, out_bias, layer_scale, x):
    qq = mxq(f64(queries).reshape(H * T, D), 1, "e4m3")
    scores = (qq @ unpack4(kt_words, kt_scales)).reshape(H, T, S)
    z = scores + f64(score_bias)[:, None, :]
    a = f64(key_gain)[:, None, :] / (1.0 + np.exp(-z))
    aq = mxq(a.transpose(1, 0, 2).reshape(T, H * S), 1, "e4m3")
    o = aq @ unpack4(vo_words, vo_scales)
    y = f64(x) + f64(layer_scale) * (o + f64(out_bias))
    Y = y.T
    words, scales = planes(Y)
    return y, words, scales

@@ -1,0 +1,415 @@
+from contextlib import ExitStack
+
+import concourse.mybir as mybir
+from concourse.masks import make_identity
+
+H, T, D, S, E = 4, 512, 512, 1024, 1024
+FLOPS = 2 * H * T * D * S + 2 * T * H * S * E
+
+F32 = mybir.dt.float32
+BF16 = mybir.dt.bfloat16
+U32 = mybir.dt.uint32
+I32 = mybir.dt.int32
+U8 = mybir.dt.uint8
+FP8X4 = mybir.dt.float8_e4m3fn_x4
+FP4X4 = mybir.dt.float4_e2m1fn_x4
+ACT = mybir.ActivationFunctionType
+ALU = mybir.AluOpType
+
+P = 128
+RUN = 2
+CHUNKS = [256, 256]
+GAIN_IN_PSUM = True
+NEED_GAIN = False
+Y_GROUPS = [[(0, 0), (1, 0)], [(0, 1), (1, 1)], [(2, 0), (3, 0)], [(2, 1), (3, 1)]]
+LOADS = [('lktw', 0, 1), ('lq', 0), ('lkts', 0), ('lrows', 0), ('lq', 1), ('lktw', 1, 2), ('lq', 2), ('lq', 3), ('lvos', 0), ('lvo', 0, 0), ('lvo', 0, 1), ('lls',), ('lob',), ('lq', 4), ('lq', 5), ('lx', 0), ('lvos', 1), ('lvo', 1, 0), ('lq', 6), ('lq', 7), ('lvo', 1, 1), ('lx', 1)]
+ORDER = [
+    ('qT', 0, 4), ('pw', 0), ('rT', 7), ('qC', 0, False), ('qT', 1, 5),
+    ('ps', 0), ('qQ', 0), ('s1', 0, 0, 0, 1, 6), ('rC',), ('sg', 0, 0, 0),
+    ('qC', 1, True), ('s1', 0, 1, 0, 1, 4), ('qQ', 1), ('s1', 0, 2, 0, 1, 5), ('sg', 0, 1, 0),
+    ('s1', 0, 3, 0, 1, 6), ('pw', 1), ('sg', 0, 3, 0), ('sg', 0, 2, 0), ('qT', 2, 4),
+    ('qC', 2, False), ('s1', 0, 0, 1, 2, 6), ('s1', 0, 1, 1, 2, 5), ('s1', 0, 2, 1, 2, 4), ('ps', 1),
+    ('sg', 0, 0, 1), ('sg', 0, 1, 1), ('sg', 0, 2, 1), ('s1', 0, 3, 1, 2, 6), ('sg', 0, 3, 1),
+    ('mu', 0, 0), ('s1', 1, 0, 0, 2, 5), ('aQ', 0, 0, 2), ('sg', 1, 0, 0), ('mu', 0, 1),
+    ('qT', 3, 4), ('sg', 1, 0, 1), ('s1', 1, 1, 0, 2, 6), ('s1', 1, 2, 0, 2, 5), ('qC', 3, False),
+    ('qQ', 2), ('aQ', 0, 2, 4), ('sg', 1, 1, 0), ('s2', 0, 0, 0, 0, 0, True, False), ('s1', 1, 3, 0, 2, 4),
+    ('sg', 1, 1, 1), ('qQ', 3), ('sg', 1, 2, 0), ('sg', 1, 3, 0), ('s2', 0, 0, 1, 1, 3, True, False),
+    ('s2', 0, 0, 1, 0, 2, True, False), ('s1', 2, 0, 0, 2, 6), ('mu', 1, 0), ('sg', 1, 3, 1), ('sg', 1, 2, 1),
+    ('s2', 0, 0, 0, 1, 1, True, False), ('sg', 2, 0, 0), ('s1', 2, 1, 0, 2, 4), ('sg', 2, 0, 1), ('sg', 2, 1, 0),
+    ('s2', 0, 1, 0, 0, 0, False, False), ('s1', 2, 2, 0, 2, 5), ('s2', 0, 1, 1, 0, 2, False, False), ('sg', 2, 1, 1), ('s1', 2, 3, 0, 2, 6),
+    ('sg', 2, 2, 0), ('s2', 0, 1, 0, 1, 1, False, False), ('mu', 1, 1), ('sg', 2, 2, 1), ('aQ', 1, 0, 2),
+    ('s2', 0, 1, 1, 1, 3, False, False), ('sg', 2, 3, 1), ('sg', 2, 3, 0), ('s1', 3, 0, 0, 2, 4), ('sg', 3, 0, 1),
+    ('sg', 3, 0, 0), ('aQ', 1, 2, 4), ('qT', 4, 5), ('qT', 5, 6), ('s1', 3, 1, 0, 2, 4),
+    ('mu', 2, 1), ('qC', 4, False), ('mu', 2, 0), ('s2', 1, 0, 1, 0, 2, False, False), ('s1', 3, 2, 0, 2, 5),
+    ('qC', 5, False), ('s2', 1, 0, 0, 0, 0, False, False), ('sg', 3, 1, 0), ('s2', 1, 1, 1, 0, 2, False, False), ('s1', 3, 3, 0, 2, 6),
+    ('qQ', 5), ('s2', 1, 0, 0, 1, 1, False, False), ('qQ', 4), ('sg', 3, 2, 1), ('s2', 1, 0, 1, 1, 3, False, False),
+    ('aQ', 2, 0, 2), ('sg', 3, 2, 0), ('aQ', 2, 2, 4), ('lsb', 1), ('s1', 4, 0, 0, 2, 5),
+    ('sg', 3, 3, 0), ('sg', 3, 3, 1), ('s2', 1, 1, 1, 1, 3, False, False), ('s1', 4, 1, 0, 2, 6), ('mu', 3, 0),
+    ('sg', 3, 1, 1), ('xb', 0, 2), ('sg', 4, 0, 0), ('s1', 4, 2, 0, 2, 4), ('sg', 4, 0, 1),
+    ('s2', 2, 0, 1, 0, 2, False, False), ('s1', 4, 3, 0, 2, 5), ('s2', 2, 0, 1, 1, 3, False, False), ('mu', 3, 1), ('s2', 2, 1, 1, 0, 2, False, False),
+    ('sg', 4, 1, 0), ('aQ', 3, 0, 2), ('sg', 4, 2, 1), ('sg', 4, 1, 1), ('sg', 4, 3, 1),
+    ('s2', 2, 1, 1, 1, 3, False, False), ('aQ', 3, 2, 4), ('sg', 4, 3, 0), ('qT', 7, 6), ('s2', 3, 0, 1, 1, 3, False, False),
+    ('s1', 5, 0, 0, 2, 5), ('mu', 4, 1), ('sg', 4, 2, 0), ('qC', 7, False), ('s1', 5, 1, 0, 2, 4),
+    ('s2', 3, 1, 1, 1, 3, False, True), ('s2', 3, 0, 1, 0, 2, False, False), ('mu', 4, 0), ('s2', 3, 1, 1, 0, 2, False, True), ('qT', 6, 6),
+    ('m', 1, 1), ('sg', 5, 1, 1), ('sg', 5, 1, 0), ('sg', 5, 0, 1), ('s2', 1, 1, 0, 1, 1, False, False),
+    ('sg', 5, 0, 0), ('s1', 5, 2, 0, 2, 4), ('s2', 1, 1, 0, 0, 0, False, False), ('qC', 6, False), ('s2', 2, 0, 0, 0, 0, False, False),
+    ('qQ', 7), ('aQ', 4, 0, 2), ('m', 1, 0), ('s2', 2, 1, 0, 0, 0, False, False), ('qQ', 6),
+    ('sg', 5, 2, 1), ('s1', 5, 3, 0, 2, 5), ('sg', 5, 2, 0), ('sg', 5, 3, 0), ('s2', 2, 0, 0, 1, 1, False, False),
+    ('s2', 3, 0, 0, 0, 0, False, False), ('s1', 6, 0, 0, 2, 6), ('xb', 1, 3), ('s1', 6, 1, 0, 2, 4), ('y', 1, 0, 1, 104),
+    ('s2', 3, 1, 0, 0, 0, False, True), ('aQ', 4, 2, 4), ('s2', 2, 1, 0, 1, 1, False, False), ('sg', 6, 0, 0), ('sg', 6, 0, 1),
+    ('xb', 2, 4), ('sg', 5, 3, 1), ('s2', 4, 0, 1, 0, 2, True, False), ('s2', 3, 0, 0, 1, 1, False, False), ('mu', 5, 0),
+    ('m', 0, 0), ('s2', 4, 1, 1, 0, 2, False, False), ('mu', 5, 1), ('s1', 6, 2, 0, 2, 6), ('s1', 6, 3, 0, 2, 5),
+    ('s2', 3, 1, 0, 1, 1, False, True), ('sg', 6, 1, 0), ('s2', 4, 0, 1, 1, 3, True, False), ('sg', 6, 1, 1), ('sg', 6, 2, 1),
+    ('aQ', 5, 0, 2), ('aQ', 5, 2, 4), ('sg', 6, 3, 0), ('s2', 4, 1, 1, 1, 3, False, False), ('s1', 7, 0, 0, 2, 4),
+    ('sg', 6, 3, 1), ('s2', 4, 0, 0, 0, 0, True, False), ('sg', 6, 2, 0), ('sg', 7, 0, 0), ('s2', 5, 0, 1, 0, 2, False, False),
+    ('mu', 6, 1), ('s1', 7, 1, 0, 2, 5), ('s2', 5, 0, 1, 1, 3, False, False), ('m', 0, 1), ('s1', 7, 2, 0, 2, 6),
+    ('xb', 3, 5), ('sg', 7, 0, 1), ('s2', 4, 1, 0, 0, 0, False, False), ('s1', 7, 3, 0, 2, 4), ('sg', 7, 1, 1),
+    ('sg', 7, 2, 0), ('s2', 5, 1, 1, 1, 3, False, False), ('sg', 7, 3, 1), ('sg', 7, 3, 0), ('s2', 4, 0, 0, 1, 1, True, False),
+    ('mu', 6, 0), ('s2', 5, 0, 0, 0, 0, False, False), ('s2', 5, 1, 0, 0, 0, False, False), ('s2', 4, 1, 0, 1, 1, False, False), ('s2', 5, 1, 1, 0, 2, False, False),
+    ('sg', 7, 1, 0), ('s2', 5, 0, 0, 1, 1, False, False), ('aQ', 6, 2, 4), ('s2', 5, 1, 0, 1, 1, False, False), ('sg', 7, 2, 1),
+    ('aQ', 6, 0, 2), ('mu', 7, 0), ('mu', 7, 1), ('aQ', 7, 0, 2), ('s2', 6, 0, 0, 1, 1, False, False),
+    ('y', 0, 0, 2, 6), ('s2', 6, 0, 0, 0, 0, False, False), ('s2', 6, 0, 1, 0, 2, False, False), ('yR', 0, 1), ('s2', 6, 1, 0, 1, 1, False, False),
+    ('s2', 6, 1, 1, 0, 2, False, False), ('s2', 6, 1, 0, 0, 0, False, False), ('s2', 6, 0, 1, 1, 3, False, False), ('yR', 0, 0), ('aQ', 7, 2, 4),
+    ('s2', 7, 0, 0, 0, 0, False, False), ('s2', 7, 1, 0, 0, 0, False, True), ('s2', 7, 0, 1, 0, 2, False, False), ('y', 1, 1, 2, 104), ('m', 2, 0),
+    ('yR', 1, 0), ('s2', 7, 1, 1, 0, 2, False, True), ('m', 3, 0), ('s2', 7, 0, 0, 1, 1, False, False), ('yR', 1, 1),
+    ('s2', 6, 1, 1, 1, 3, False, False), ('s2', 7, 1, 0, 1, 1, False, True), ('yT', 0, 4), ('y', 2, 0, 1, 107), ('s2', 7, 0, 1, 1, 3, False, False),
+    ('s2', 7, 1, 1, 1, 3, False, True), ('y', 3, 0, 1, 110), ('m', 2, 1), ('m', 3, 1), ('yT', 1, 5),
+    ('yC', 0, False), ('yR', 2, 0), ('y', 2, 1, 2, 107), ('yC', 1, False), ('y', 3, 1, 2, 110),
+    ('yR', 3, 0), ('yQ', 0), ('yR', 2, 1), ('yQ', 1), ('yT', 2, 6),
+    ('yR', 3, 1), ('yC', 2, False), ('yT', 3, 4), ('yQ', 2), ('yC', 3, False),
+    ('yQ', 3),
+]
+
+
+def tile_sigmoid_attention_folded_output_h1_kernel(
+    tc, queries, kt_words, kt_scales, score_bias, key_gain, vo_words, vo_scales,
+    out_bias, layer_scale, x, out_0, out_1, out_2,
+):
+    nc = tc.nc
+    starts = [sum(CHUNKS[:c]) for c in range(len(CHUNKS))]
+    units = []
+    for c, n in enumerate(CHUNKS):
+        for hg in range(H * n // 512):
+            for g in range(2):
+                units.append((c, hg, g))
+    tiles = [(c, j) for c, n in enumerate(CHUNKS) for j in range(n // P)]
+
+    with ExitStack() as ctx:
+        keep = ctx.enter_context(tc.tile_pool(name="keep", bufs=1))
+        work = ctx.enter_context(tc.tile_pool(name="work", bufs=2))
+        psum = ctx.enter_context(tc.psum_pool(name="psum", bufs=1))
+        ctx.enter_context(tc.manual_schedule())
+
+        def kept(name, shape, dtype):
+            return keep.tile(shape, dtype, name=name, align_bytes=64)
+
+        warm_in = kept("warm_in", [P, 8], F32)
+        warm_out = kept("warm_out", [P, 8], F32)
+        ident_f32 = kept("ident_f32", [P, P], F32)
+        ident_bf16 = kept("ident_bf16", [P, P], BF16)
+        ktw_raw = kept("ktw_raw", [P, 2 * S], U8)
+        kts_raw = kept("kts_raw", [P, S], U8)
+        ktw = kept("ktw", [P, 2 * S], U8)
+        kts = kept("kts", [P, S], U8)
+        key_rows = kept("key_rows", [P, 512], BF16)
+        bias = kept("bias", [P, 8, 4], F32)
+        gain = kept("gain", [P, 8, 4 * RUN], F32)
+        vos = kept("vos", [P, 8, E], U8)
+        vow = {(hp, g): kept("vow%d%d" % (hp, g), [P, 2, 2 * E], U8) for hp in range(2) for g in range(2)}
+        q_raw = {b: kept("q_raw%d" % b, [P, 2, D], BF16) for b in range(8)}
+        q_codes = {b: kept("q_codes%d" % b, [P, 512], U32) for b in range(4)}
+        q_scales = {b: kept("q_scales%d" % b, [P, 512], U8) for b in range(4)}
+        ls_rows = kept("ls_rows", [P, E], BF16)
+        ob_rows = kept("ob_rows", [P, E], BF16)
+        x_sb = {i: kept("x_sb%d" % i, [P, 2, E], BF16) for i in range(2)}
+        y_codes = kept("y_codes", [P, 2, T], U32)
+        y_scales = kept("y_scales", [P, 2, T], U8)
+
+        live = {}
+
+        def bank_tile(b, shape, dtype):
+            return psum.tile(shape, dtype, name="bank", tag="bank%d" % b)
+
+        def shared(slot, shape, dtype):
+            return keep.tile(shape, dtype, name="shared", tag="slot%d" % slot, align_bytes=64)
+
+        def q_block(b):
+            k = 2 * (b // 2)
+            c, hg, g = units[k]
+            return c, hg, b % 2
+
+        def load_q(b):
+            c, hg, half = q_block(b)
+            rows = slice(starts[c], starts[c] + CHUNKS[c])
+            if CHUNKS[c] == 256:
+                src = queries[2 * hg + half, rows, :].rearrange("(p n) d -> p n d", n=2)
+            else:
+                src = queries[2 * half:2 * half + 2, rows, :].rearrange("n p d -> p n d")
+            nc.sync.dma_start(out=q_raw[b][:], in_=src)
+
+        def load_vo(hp, g):
+            nc.sync.dma_start(
+                out=vow[hp, g][:].bitcast(I32),
+                in_=vo_words[4 * hp + g:4 * hp + 4:2].rearrange("k p n -> p k n").bitcast(I32))
+
+        def load_x(i):
+            nc.sync.dma_start(
+                out=x_sb[i][:], in_=x[i * 256:(i + 1) * 256, :].rearrange("(j p) e -> p j e", j=2))
+
+        def load_ktw(lo, hi):
+            cols = slice(lo * 1024, hi * 1024)
+            nc.sync.dma_start(out=ktw_raw[:, cols].bitcast(I32), in_=kt_words[0, :, cols].bitcast(I32))
+
+        def load_kts(on_scalar):
+            queue = nc.scalar if on_scalar else nc.sync
+            for quad in range(4):
+                queue.dma_start(
+                    out=kts_raw[32 * quad:32 * quad + 4, :].bitcast(I32),
+                    in_=kt_scales[0, 4 * quad:4 * quad + 4, :].bitcast(I32))
+
+        def load_rows(on_scalar):
+            queue = nc.scalar if on_scalar else nc.sync
+            queue.dma_start(out=key_rows[0:8, :], in_=score_bias.rearrange("h (g k) -> (h g) k", g=2))
+            queue.dma_start(out=key_rows[8:16, :], in_=key_gain.rearrange("h (g k) -> (h g) k", g=2))
+
+        def load_vos(hp):
+            for quad in range(4):
+                nc.sync.dma_start(
+                    out=vos[32 * quad:32 * quad + 4, 4 * hp:4 * hp + 4, :].bitcast(I32),
+                    in_=vo_scales[4 * hp:4 * hp + 4, 4 * quad:4 * quad + 4, :].rearrange("k r n -> r k n").bitcast(I32))
+
+        def load_ls():
+            nc.sync.dma_start(out=ls_rows[:], in_=layer_scale.partition_broadcast(P))
+
+        def load_ob():
+            nc.sync.dma_start(out=ob_rows[:], in_=out_bias.partition_broadcast(P))
+
+        def permute_kt_words(g):
+            cols = slice(g * 1024, (g + 1) * 1024)
+            nc.vector.tensor_copy(
+                out=ktw[:, cols].rearrange("p (t m b) -> p t m b", t=4, b=2),
+                in_=ktw_raw[:, cols].rearrange("p (m t b) -> p t m b", t=4, b=2))
+
+        def permute_kt_scales(g):
+            cols = slice(g * 512, (g + 1) * 512)
+            nc.vector.tensor_copy(
+                out=kts[:, cols].rearrange("p (t m) -> p t m", t=4),
+                in_=kts_raw[:, cols].rearrange("p (m t) -> p t m", t=4))
+
+        def turn_key_rows(bk):
+            bank = bank_tile(bk, [P, 4, P], BF16)
+            for t in range(4):
+                nc.tensor.transpose(bank[:, t, :], key_rows[:, t:512:4], ident_bf16[:])
+            live["rows"] = bank
+
+        def take_key_rows():
+            bank = live["rows"]
+            nc.vector.tensor_copy(out=bias[:], in_=bank[:, :, 0:8].rearrange("p t r -> p r t"))
+            if NEED_GAIN:
+                nc.vector.tensor_copy(
+                    out=gain[:].rearrange("p r (t i) -> p r t i", i=RUN),
+                    in_=bank[:, :, 8:16].rearrange("p t r -> p r t").unsqueeze(3).to_broadcast([P, 8, 4, RUN]))
+
+        def turn_q(b, bk):
+            bank = bank_tile(bk, [P, 4, P], F32)
+            words = q_raw[b][:].bitcast(F32)
+            for n in range(2):
+                for u in range(2):
+                    nc.tensor.transpose(bank[:, 2 * n + u, :], words[:, n, u:256:2], ident_f32[:])
+            live["qbank", b] = bank
+
+        def copy_q(b, on_vector):
+            grouped = work.tile([P, 1024], BF16, name="q_grouped", bufs=4, align_bytes=64)
+            if CHUNKS[q_block(b)[0]] == 256:
+                dst = grouped[:].bitcast(F32).rearrange("p (r w) -> p r w", w=4)
+                src = live["qbank", b][:].rearrange("p w r -> p r w")
+            else:
+                dst = grouped[:].bitcast(F32).rearrange("p (n r u) -> p n r u", n=2, u=2)
+                src = live["qbank", b][:].rearrange("p (n u) r -> p n r u", n=2)
+            if on_vector:
+                nc.vector.tensor_copy(out=dst, in_=src)
+            else:
+                nc.scalar.copy(out=dst, in_=src)
+            live["qg", b] = grouped
+
+        def quant_q(b):
+            cols = slice((b % 2) * 256, (b % 2 + 1) * 256)
+            nc.vector.quantize_mx(
+                out=q_codes[b // 2][:, cols].bitcast(FP8X4), scales=q_scales[b // 2][:, cols], in_=live["qg", b][:])
+
+        def pass_of(k, hh):
+            c, hg, g = units[k]
+            return 2 * (hg * 512 // CHUNKS[c] + hh) + g
+
+        def scores(k, t, lo, hi, bk):
+            c, hg, g = units[k]
+            bank = bank_tile(bk, [P, 512], F32)
+            slot = 4 * g + t
+            cols = slice(lo * 256, hi * 256)
+            nc.tensor.matmul_mx(
+                out=bank[:, cols],
+                lhsT=ktw[:, slot * 256:(slot + 1) * 256].bitcast(FP4X4),
+                lhsT_scale=kts[:, slot * 128:(slot + 1) * 128],
+                rhs=q_codes[k // 2][:, cols].bitcast(FP8X4),
+                rhs_scale=q_scales[k // 2][:, cols],
+                start=True, stop=True)
+            for half in range(lo, hi):
+                live["s", k, t, half] = bank
+
+        def sigmoid(k, t, hh):
+            n = CHUNKS[units[k][0]]
+            if ("sig", k) not in live:
+                live["sig", k] = work.tile([P, 512 // n, 4, n], F32, name="sig", bufs=3)
+            nc.scalar.activation(
+                out=live["sig", k][:, hh, t, :], in_=live["s", k, t, hh * n // 256][:, hh * n:(hh + 1) * n],
+                func=ACT.Sigmoid, bias=bias[:, pass_of(k, hh), t:t + 1])
+
+        def apply_gain(k, hh):
+            n = CHUNKS[units[k][0]]
+            row = pass_of(k, hh)
+            if ("a", k) not in live:
+                live["a", k] = shared(k, [P, 2048], BF16)
+            if GAIN_IN_PSUM:
+                gains = live["rows"][:, :, 8 + row:9 + row].unsqueeze(1)
+            else:
+                gains = gain[:, row, :].rearrange("p (t i) -> p t i", i=RUN).unsqueeze(1)
+            nc.vector.tensor_tensor(
+                out=live["a", k][:, hh * 4 * n:(hh + 1) * 4 * n].rearrange("p (c i t) -> p c t i", i=RUN, t=4),
+                in0=live["sig", k][:, hh].rearrange("p t (c i) -> p c t i", i=RUN),
+                in1=gains.to_broadcast([P, n // RUN, 4, RUN]),
+                op=ALU.mult)
+
+        def gain_rows(k, hh, t):
+            n = CHUNKS[units[k][0]]
+            if ("ar", k, hh) not in live:
+                live["ar", k, hh] = work.tile([P, 4, n], BF16, name="a_rows", bufs=2, align_bytes=64)
+            nc.scalar.activation(
+                out=live["ar", k, hh][:, t, :], in_=live["sig", k][:, hh, t, :], func=ACT.Copy,
+                scale=gain[:, pass_of(k, hh), RUN * t:RUN * t + 1])
+
+        def interleave(k, hh):
+            n = CHUNKS[units[k][0]]
+            if ("a", k) not in live:
+                live["a", k] = shared(k, [P, 2048], BF16)
+            nc.vector.tensor_copy(
+                out=live["a", k][:, hh * 4 * n:(hh + 1) * 4 * n].rearrange("p (c i t) -> p c t i", i=4, t=4),
+                in_=live["ar", k, hh][:].rearrange("p t (c i) -> p c t i", i=4))
+
+        def quant_a(k, lo, hi):
+            if ("aq", k) not in live:
+                codes = work.tile([P, 512], U32, name="a_codes", bufs=4, align_bytes=64)
+                scales = work.tile([P, 512], U8, name="a_scales", bufs=4, align_bytes=64)
+                live["aq", k] = (codes, scales)
+            codes, scales = live["aq", k]
+            nc.vector.quantize_mx(
+                out=codes[:, lo * P:hi * P].bitcast(FP8X4), scales=scales[:, lo * P:hi * P],
+                in_=live["a", k][:, lo * 512:hi * 512])
+
+        def project(k, hh, j, eg, bk, first, last):
+            c, hg, g = units[k]
+            codes, scales = live["aq", k]
+            row = pass_of(k, hh)
+            if first:
+                live["acc", c, j, eg] = bank_tile(bk, [P, 512], F32)
+            cols = slice(hh * CHUNKS[c] + j * P, hh * CHUNKS[c] + (j + 1) * P)
+            nc.tensor.matmul_mx(
+                out=live["acc", c, j, eg][:],
+                lhsT=codes[:, cols].bitcast(FP8X4),
+                lhsT_scale=scales[:, cols],
+                rhs=vow[row // 4, g][:, (row // 2) % 2, eg * 1024:(eg + 1) * 1024].bitcast(FP4X4),
+                rhs_scale=vos[:, row, eg * 512:(eg + 1) * 512],
+                start=first, stop=last)
+
+        def engine(slot):
+            return nc.vector if slot >= 100 else nc.gpsimd
+
+        def make_lsb(slot):
+            live["lsb"] = shared(slot, [P, E], F32)
+            engine(slot).tensor_tensor(out=live["lsb"][:], in0=ls_rows[:], in1=ob_rows[:], op=ALU.mult)
+
+        def make_xb(i, slot):
+            live["xb", i] = shared(slot, [P, E], F32)
+            engine(slot).tensor_tensor(
+                out=live["xb", i][:], in0=x_sb[i // 2][:, i % 2, :], in1=live["lsb"][:], op=ALU.add)
+
+        def scale_o(i, eg):
+            c, j = tiles[i]
+            if ("m", i) not in live:
+                live["m", i] = work.tile([P, E], F32, name="m", bufs=2)
+            cols = slice(eg * 512, (eg + 1) * 512)
+            nc.vector.tensor_tensor(
+                out=live["m", i][:, cols], in0=live["acc", c, j, eg][:], in1=ls_rows[:, cols], op=ALU.mult)
+
+        def finish_y(i, lo, hi, slot):
+            if ("y", i) not in live:
+                live["y", i] = shared(slot, [P, E], F32)
+            cols = slice(lo * 512, hi * 512)
+            engine(slot).tensor_tensor(
+                out=live["y", i][:, cols], in0=live["m", i][:, cols], in1=live["xb", i][:, cols], op=ALU.add)
+            nc.sync.dma_start(out=out_0[i * P:(i + 1) * P, cols], in_=live["y", i][:, cols])
+
+        def round_y(i, eg):
+            y16 = work.tile([P, 512], BF16, name="y16", bufs=4, align_bytes=64)
+            nc.scalar.copy(
+                out=y16[:].rearrange("p (u q i) -> p u q i", u=2, i=2),
+                in_=live["y", i][:, eg * 512:(eg + 1) * 512].rearrange("p (q u i) -> p u q i", u=2, i=2))
+            live["y16", i, eg] = y16
+
+        def turn_y(grp, bk):
+            pieces = Y_GROUPS[grp]
+            bank = bank_tile(bk, [P, 2 * len(pieces), P], F32)
+            for s, (i, eg) in enumerate(pieces):
+                words = live["y16", i, eg][:].bitcast(F32)
+                for u in range(2):
+                    nc.tensor.transpose(bank[:, 2 * s + u, :], words[:, u * P:(u + 1) * P], ident_f32[:])
+            live["ybank", grp] = bank
+
+        def copy_y(grp, on_vector):
+            pieces = Y_GROUPS[grp]
+            grouped = work.tile([P, 512 * len(pieces)], BF16, name="y_grouped", bufs=2, align_bytes=64)
+            dst = grouped[:].bitcast(F32).rearrange("p (s r u) -> p s r u", r=P, u=2)
+            src = live["ybank", grp][:].rearrange("p (s u) r -> p s r u", u=2)
+            if on_vector:
+                nc.vector.tensor_copy(out=dst, in_=src)
+            else:
+                nc.scalar.copy(out=dst, in_=src)
+            live["yg", grp] = grouped
+
+        def quant_y(grp):
+            pieces = Y_GROUPS[grp]
+            i, eg = pieces[0]
+            cols = slice(i * P, (i + len(pieces)) * P)
+            nc.vector.quantize_mx(
+                out=y_codes[:, eg, cols].bitcast(FP8X4), scales=y_scales[:, eg, cols], in_=live["yg", grp][:])
+            nc.sync.dma_start(
+                out=out_1[eg].rearrange("p m t -> p (m t)")[:, 4 * cols.start:4 * cols.stop].bitcast(I32),
+                in_=y_codes[:, eg, cols].bitcast(I32))
+
+        def store_y_scales():
+            for quad in range(4):
+                queue = nc.sync if quad % 2 == 0 else nc.scalar
+                queue.dma_start(
+                    out=out_2[:, 4 * quad:4 * quad + 4, :].rearrange("g r m -> r g m").bitcast(I32),
+                    in_=y_scales[32 * quad:32 * quad + 4, :, :].bitcast(I32))
+
+        steps = {
+            "lq": load_q, "lvo": load_vo, "lx": load_x, "lktw": load_ktw, "lkts": load_kts, "lrows": load_rows,
+            "lvos": load_vos, "lls": load_ls, "lob": load_ob,
+            "pw": permute_kt_words, "ps": permute_kt_scales, "rT": turn_key_rows, "rC": take_key_rows,
+            "qT": turn_q, "qC": copy_q, "qQ": quant_q, "s1": scores, "sg": sigmoid, "mu": apply_gain,
+            "aQ": quant_a, "ga": gain_rows, "il": interleave, "s2": project, "lsb": make_lsb, "xb": make_xb, "m": scale_o, "y": finish_y,
+            "yR": round_y, "yT": turn_y, "yC": copy_y, "yQ": quant_y,
+        }
+
+        nc.vector.memset(kts_raw[:].bitcast(I32), 0)
+        nc.vector.memset(key_rows[:], 0.0)
+        nc.vector.memset(warm_in[:], 0.0)
+        nc.vector.memset(vos[:].rearrange("p k n -> p (k n)").bitcast(I32), 0)
+        make_identity(nc, ident_f32[:])
+        make_identity(nc, ident_bf16[:])
+        for step in LOADS:
+            steps[step[0]](*step[1:])
+        nc.scalar.activation(out=warm_out[:], in_=warm_in[:], func=ACT.Sigmoid)
+        for step in ORDER:
+            steps[step[0]](*step[1:])
+        store_y_scales()

@@ -18,66 +18,76 @@ ALU = mybir.AluOpType
 
 P = 128
 RUN = 2
-CHUNKS = [256, 256]
+CHUNKS = [256, 128, 128]
 GAIN_IN_PSUM = True
 NEED_GAIN = False
-Y_GROUPS = [[(0, 0), (1, 0)], [(0, 1), (1, 1)], [(2, 0), (3, 0)], [(2, 1), (3, 1)]]
-LOADS = [('lktw', 0, 1), ('lq', 0), ('lkts', 0), ('lrows', 0), ('lq', 1), ('lktw', 1, 2), ('lq', 2), ('lq', 3), ('lvos', 0), ('lvo', 0, 0), ('lvo', 0, 1), ('lls',), ('lob',), ('lq', 4), ('lq', 5), ('lx', 0), ('lvos', 1), ('lvo', 1, 0), ('lq', 6), ('lq', 7), ('lvo', 1, 1), ('lx', 1)]
+Y_GROUPS = [[(0, 0), (1, 0)], [(0, 1), (1, 1)], [(2, 0)], [(2, 1)], [(3, 0)], [(3, 1)]]
+LOADS = [('lktw', 0, 1), ('lq', 0), ('lkts', 0), ('lrows', 0), ('lq', 1), ('lktw', 1, 2), ('lq', 2), ('lq', 3), ('lls',), ('lob',), ('lvos', 0), ('lvo', 0, 0), ('lq', 4), ('lq', 5), ('lvo', 0, 1), ('lx', 0), ('lvos', 1), ('lvo', 1, 0), ('lq', 6), ('lq', 7), ('lvo', 1, 1), ('lx', 1), ('lbc',)]
 ORDER = [
-    ('qT', 0, 4), ('pw', 0), ('rT', 7), ('qC', 0, False), ('qT', 1, 5),
-    ('ps', 0), ('qQ', 0), ('s1', 0, 0, 0, 1, 6), ('rC',), ('sg', 0, 0, 0),
-    ('qC', 1, True), ('s1', 0, 1, 0, 1, 4), ('qQ', 1), ('s1', 0, 2, 0, 1, 5), ('sg', 0, 1, 0),
-    ('s1', 0, 3, 0, 1, 6), ('pw', 1), ('sg', 0, 3, 0), ('sg', 0, 2, 0), ('qT', 2, 4),
-    ('qC', 2, False), ('s1', 0, 0, 1, 2, 6), ('s1', 0, 1, 1, 2, 5), ('s1', 0, 2, 1, 2, 4), ('ps', 1),
-    ('sg', 0, 0, 1), ('sg', 0, 1, 1), ('sg', 0, 2, 1), ('s1', 0, 3, 1, 2, 6), ('sg', 0, 3, 1),
-    ('mu', 0, 0), ('s1', 1, 0, 0, 2, 5), ('aQ', 0, 0, 2), ('sg', 1, 0, 0), ('mu', 0, 1),
-    ('qT', 3, 4), ('sg', 1, 0, 1), ('s1', 1, 1, 0, 2, 6), ('s1', 1, 2, 0, 2, 5), ('qC', 3, False),
-    ('qQ', 2), ('aQ', 0, 2, 4), ('sg', 1, 1, 0), ('s2', 0, 0, 0, 0, 0, True, False), ('s1', 1, 3, 0, 2, 4),
-    ('sg', 1, 1, 1), ('qQ', 3), ('sg', 1, 2, 0), ('sg', 1, 3, 0), ('s2', 0, 0, 1, 1, 3, True, False),
-    ('s2', 0, 0, 1, 0, 2, True, False), ('s1', 2, 0, 0, 2, 6), ('mu', 1, 0), ('sg', 1, 3, 1), ('sg', 1, 2, 1),
-    ('s2', 0, 0, 0, 1, 1, True, False), ('sg', 2, 0, 0), ('s1', 2, 1, 0, 2, 4), ('sg', 2, 0, 1), ('sg', 2, 1, 0),
-    ('s2', 0, 1, 0, 0, 0, False, False), ('s1', 2, 2, 0, 2, 5), ('s2', 0, 1, 1, 0, 2, False, False), ('sg', 2, 1, 1), ('s1', 2, 3, 0, 2, 6),
-    ('sg', 2, 2, 0), ('s2', 0, 1, 0, 1, 1, False, False), ('mu', 1, 1), ('sg', 2, 2, 1), ('aQ', 1, 0, 2),
-    ('s2', 0, 1, 1, 1, 3, False, False), ('sg', 2, 3, 1), ('sg', 2, 3, 0), ('s1', 3, 0, 0, 2, 4), ('sg', 3, 0, 1),
-    ('sg', 3, 0, 0), ('aQ', 1, 2, 4), ('qT', 4, 5), ('qT', 5, 6), ('s1', 3, 1, 0, 2, 4),
-    ('mu', 2, 1), ('qC', 4, False), ('mu', 2, 0), ('s2', 1, 0, 1, 0, 2, False, False), ('s1', 3, 2, 0, 2, 5),
-    ('qC', 5, False), ('s2', 1, 0, 0, 0, 0, False, False), ('sg', 3, 1, 0), ('s2', 1, 1, 1, 0, 2, False, False), ('s1', 3, 3, 0, 2, 6),
-    ('qQ', 5), ('s2', 1, 0, 0, 1, 1, False, False), ('qQ', 4), ('sg', 3, 2, 1), ('s2', 1, 0, 1, 1, 3, False, False),
-    ('aQ', 2, 0, 2), ('sg', 3, 2, 0), ('aQ', 2, 2, 4), ('lsb', 1), ('s1', 4, 0, 0, 2, 5),
-    ('sg', 3, 3, 0), ('sg', 3, 3, 1), ('s2', 1, 1, 1, 1, 3, False, False), ('s1', 4, 1, 0, 2, 6), ('mu', 3, 0),
-    ('sg', 3, 1, 1), ('xb', 0, 2), ('sg', 4, 0, 0), ('s1', 4, 2, 0, 2, 4), ('sg', 4, 0, 1),
-    ('s2', 2, 0, 1, 0, 2, False, False), ('s1', 4, 3, 0, 2, 5), ('s2', 2, 0, 1, 1, 3, False, False), ('mu', 3, 1), ('s2', 2, 1, 1, 0, 2, False, False),
-    ('sg', 4, 1, 0), ('aQ', 3, 0, 2), ('sg', 4, 2, 1), ('sg', 4, 1, 1), ('sg', 4, 3, 1),
-    ('s2', 2, 1, 1, 1, 3, False, False), ('aQ', 3, 2, 4), ('sg', 4, 3, 0), ('qT', 7, 6), ('s2', 3, 0, 1, 1, 3, False, False),
-    ('s1', 5, 0, 0, 2, 5), ('mu', 4, 1), ('sg', 4, 2, 0), ('qC', 7, False), ('s1', 5, 1, 0, 2, 4),
-    ('s2', 3, 1, 1, 1, 3, False, True), ('s2', 3, 0, 1, 0, 2, False, False), ('mu', 4, 0), ('s2', 3, 1, 1, 0, 2, False, True), ('qT', 6, 6),
-    ('m', 1, 1), ('sg', 5, 1, 1), ('sg', 5, 1, 0), ('sg', 5, 0, 1), ('s2', 1, 1, 0, 1, 1, False, False),
-    ('sg', 5, 0, 0), ('s1', 5, 2, 0, 2, 4), ('s2', 1, 1, 0, 0, 0, False, False), ('qC', 6, False), ('s2', 2, 0, 0, 0, 0, False, False),
-    ('qQ', 7), ('aQ', 4, 0, 2), ('m', 1, 0), ('s2', 2, 1, 0, 0, 0, False, False), ('qQ', 6),
-    ('sg', 5, 2, 1), ('s1', 5, 3, 0, 2, 5), ('sg', 5, 2, 0), ('sg', 5, 3, 0), ('s2', 2, 0, 0, 1, 1, False, False),
-    ('s2', 3, 0, 0, 0, 0, False, False), ('s1', 6, 0, 0, 2, 6), ('xb', 1, 3), ('s1', 6, 1, 0, 2, 4), ('y', 1, 0, 1, 104),
-    ('s2', 3, 1, 0, 0, 0, False, True), ('aQ', 4, 2, 4), ('s2', 2, 1, 0, 1, 1, False, False), ('sg', 6, 0, 0), ('sg', 6, 0, 1),
-    ('xb', 2, 4), ('sg', 5, 3, 1), ('s2', 4, 0, 1, 0, 2, True, False), ('s2', 3, 0, 0, 1, 1, False, False), ('mu', 5, 0),
-    ('m', 0, 0), ('s2', 4, 1, 1, 0, 2, False, False), ('mu', 5, 1), ('s1', 6, 2, 0, 2, 6), ('s1', 6, 3, 0, 2, 5),
-    ('s2', 3, 1, 0, 1, 1, False, True), ('sg', 6, 1, 0), ('s2', 4, 0, 1, 1, 3, True, False), ('sg', 6, 1, 1), ('sg', 6, 2, 1),
-    ('aQ', 5, 0, 2), ('aQ', 5, 2, 4), ('sg', 6, 3, 0), ('s2', 4, 1, 1, 1, 3, False, False), ('s1', 7, 0, 0, 2, 4),
-    ('sg', 6, 3, 1), ('s2', 4, 0, 0, 0, 0, True, False), ('sg', 6, 2, 0), ('sg', 7, 0, 0), ('s2', 5, 0, 1, 0, 2, False, False),
-    ('mu', 6, 1), ('s1', 7, 1, 0, 2, 5), ('s2', 5, 0, 1, 1, 3, False, False), ('m', 0, 1), ('s1', 7, 2, 0, 2, 6),
-    ('xb', 3, 5), ('sg', 7, 0, 1), ('s2', 4, 1, 0, 0, 0, False, False), ('s1', 7, 3, 0, 2, 4), ('sg', 7, 1, 1),
-    ('sg', 7, 2, 0), ('s2', 5, 1, 1, 1, 3, False, False), ('sg', 7, 3, 1), ('sg', 7, 3, 0), ('s2', 4, 0, 0, 1, 1, True, False),
-    ('mu', 6, 0), ('s2', 5, 0, 0, 0, 0, False, False), ('s2', 5, 1, 0, 0, 0, False, False), ('s2', 4, 1, 0, 1, 1, False, False), ('s2', 5, 1, 1, 0, 2, False, False),
-    ('sg', 7, 1, 0), ('s2', 5, 0, 0, 1, 1, False, False), ('aQ', 6, 2, 4), ('s2', 5, 1, 0, 1, 1, False, False), ('sg', 7, 2, 1),
-    ('aQ', 6, 0, 2), ('mu', 7, 0), ('mu', 7, 1), ('aQ', 7, 0, 2), ('s2', 6, 0, 0, 1, 1, False, False),
-    ('y', 0, 0, 2, 6), ('s2', 6, 0, 0, 0, 0, False, False), ('s2', 6, 0, 1, 0, 2, False, False), ('yR', 0, 1), ('s2', 6, 1, 0, 1, 1, False, False),
-    ('s2', 6, 1, 1, 0, 2, False, False), ('s2', 6, 1, 0, 0, 0, False, False), ('s2', 6, 0, 1, 1, 3, False, False), ('yR', 0, 0), ('aQ', 7, 2, 4),
-    ('s2', 7, 0, 0, 0, 0, False, False), ('s2', 7, 1, 0, 0, 0, False, True), ('s2', 7, 0, 1, 0, 2, False, False), ('y', 1, 1, 2, 104), ('m', 2, 0),
-    ('yR', 1, 0), ('s2', 7, 1, 1, 0, 2, False, True), ('m', 3, 0), ('s2', 7, 0, 0, 1, 1, False, False), ('yR', 1, 1),
-    ('s2', 6, 1, 1, 1, 3, False, False), ('s2', 7, 1, 0, 1, 1, False, True), ('yT', 0, 4), ('y', 2, 0, 1, 107), ('s2', 7, 0, 1, 1, 3, False, False),
-    ('s2', 7, 1, 1, 1, 3, False, True), ('y', 3, 0, 1, 110), ('m', 2, 1), ('m', 3, 1), ('yT', 1, 5),
-    ('yC', 0, False), ('yR', 2, 0), ('y', 2, 1, 2, 107), ('yC', 1, False), ('y', 3, 1, 2, 110),
-    ('yR', 3, 0), ('yQ', 0), ('yR', 2, 1), ('yQ', 1), ('yT', 2, 6),
-    ('yR', 3, 1), ('yC', 2, False), ('yT', 3, 4), ('yQ', 2), ('yC', 3, False),
-    ('yQ', 3),
+    ('qT', 0, 0), ('pw', 0), ('rT', 7), ('ps', 0), ('qT', 1, 1),
+    ('ps', 1), ('qC', 0, False), ('qQ', 0), ('qC', 1, False), ('rC',),
+    ('s1', 0, 0, 0, 1, 2), ('s1', 0, 1, 0, 1, 3), ('pw', 1), ('s1', 0, 2, 0, 1, 4), ('s1', 0, 3, 0, 1, 5),
+    ('qQ', 1), ('sg', 0, 0, 0), ('qT', 2, 6), ('s1', 0, 0, 1, 2, 0), ('s1', 0, 1, 1, 2, 1),
+    ('col',), ('sg', 0, 2, 0), ('sg', 0, 3, 0), ('sg', 0, 1, 0), ('qC', 2, False),
+    ('s1', 0, 2, 1, 2, 2), ('s1', 0, 3, 1, 2, 4), ('sg', 0, 2, 1), ('sg', 0, 0, 1), ('qT', 3, 5),
+    ('s1', 1, 0, 0, 2, 3), ('s1', 1, 1, 0, 2, 6), ('mu', 0, 0), ('sg', 0, 1, 1), ('qC', 3, True),
+    ('qQ', 2), ('s1', 1, 2, 0, 2, 2), ('sg', 0, 3, 1), ('sg', 1, 0, 0), ('s1', 1, 3, 0, 2, 0),
+    ('sg', 1, 1, 1), ('sg', 1, 2, 1), ('bT', 1, 0, 1), ('qQ', 3), ('mu', 0, 1),
+    ('bT', 1, 1, 4), ('s1', 2, 0, 0, 2, 5), ('sg', 1, 1, 0), ('sg', 1, 0, 1), ('sg', 1, 2, 0),
+    ('s1', 2, 1, 0, 2, 6), ('sg', 1, 3, 0), ('qT', 5, 3), ('bC', 1, 1, False), ('qT', 4, 2),
+    ('aQ', 0, 0, 2), ('sg', 1, 3, 1), ('aQ', 0, 2, 4), ('qC', 5, False), ('s1', 2, 2, 0, 2, 4),
+    ('s2', 0, 0, 0, 1, 0, True, False), ('qC', 4, False), ('s1', 2, 3, 0, 2, 3), ('sg', 2, 2, 0), ('s2', 0, 0, 1, 0, 2, True, False),
+    ('mu', 1, 0), ('bC', 1, 0, True), ('s2', 0, 0, 1, 1, 1, True, False), ('sg', 2, 2, 1), ('s2', 0, 1, 0, 1, -1, False, False),
+    ('aQ', 1, 0, 2), ('qQ', 5), ('s1', 3, 0, 0, 2, 4), ('s2', 0, 1, 1, 1, -1, False, False), ('sg', 2, 3, 0),
+    ('sg', 2, 3, 1), ('sg', 2, 1, 0), ('mu', 1, 1), ('sg', 2, 1, 1), ('s1', 3, 1, 0, 2, 3),
+    ('sg', 2, 0, 1), ('sg', 2, 0, 0), ('s2', 1, 0, 0, 1, -1, False, False), ('sg', 3, 1, 0), ('qQ', 4),
+    ('s2', 0, 1, 1, 0, -1, False, False), ('aQ', 1, 2, 4), ('s1', 3, 2, 0, 2, 6), ('sg', 3, 0, 0), ('sg', 3, 1, 1),
+    ('s2', 1, 0, 1, 0, -1, False, False), ('s2', 1, 1, 1, 0, -1, False, False), ('mu', 2, 0), ('s1', 3, 3, 0, 2, 5), ('sg', 3, 2, 0),
+    ('mu', 2, 1), ('sg', 3, 0, 1), ('s2', 1, 0, 1, 1, -1, False, False), ('sg', 3, 3, 1), ('s2', 1, 1, 0, 1, -1, False, False),
+    ('s1', 4, 0, 0, 2, 3), ('sg', 3, 3, 0), ('sg', 3, 2, 1), ('aQ', 2, 0, 2), ('aQ', 2, 2, 4),
+    ('s1', 4, 1, 0, 2, 4), ('sg', 4, 0, 0), ('sg', 4, 1, 2), ('sg', 4, 0, 1), ('qT', 6, 5),
+    ('s1', 4, 2, 0, 2, 6), ('sg', 4, 1, 0), ('sg', 4, 0, 3), ('s2', 2, 0, 0, 1, -1, False, False), ('qC', 6, False),
+    ('s2', 2, 1, 0, 1, -1, False, False), ('s1', 4, 3, 0, 2, 5), ('sg', 4, 2, 2), ('sg', 4, 2, 0), ('sg', 4, 0, 2),
+    ('s2', 1, 1, 1, 1, -1, False, False), ('sg', 4, 2, 1), ('sg', 4, 1, 3), ('sg', 4, 1, 1), ('s2', 2, 0, 1, 0, -1, False, False),
+    ('mu', 3, 0), ('sg', 4, 3, 3), ('qT', 7, 3), ('mu', 3, 1), ('sg', 4, 2, 3),
+    ('s1', 5, 0, 0, 2, 4), ('sg', 4, 3, 2), ('sg', 4, 3, 1), ('s1', 5, 1, 0, 2, 6), ('qQ', 6),
+    ('aQ', 3, 2, 4), ('sg', 4, 3, 0), ('aQ', 3, 0, 2), ('s1', 5, 2, 0, 2, 5), ('qC', 7, False),
+    ('s2', 2, 1, 1, 0, -1, False, False), ('s2', 3, 0, 0, 1, -1, False, False), ('s2', 2, 0, 1, 1, -1, False, False), ('sg', 5, 1, 3), ('sg', 5, 1, 2),
+    ('sg', 5, 1, 1), ('mu', 4, 3), ('sg', 5, 2, 2), ('sg', 5, 2, 0), ('sg', 5, 1, 0),
+    ('s1', 5, 3, 0, 2, 3), ('sg', 5, 3, 3), ('s2', 3, 0, 1, 0, -1, False, False), ('sg', 5, 0, 0), ('mu', 4, 1),
+    ('s2', 3, 1, 0, 1, -1, False, True), ('sg', 5, 0, 1), ('mu', 4, 0), ('sg', 5, 0, 2), ('sg', 5, 3, 0),
+    ('s2', 0, 0, 0, 0, 6, True, False), ('mu', 4, 2), ('sg', 5, 3, 2), ('sg', 5, 0, 3), ('sg', 5, 3, 1),
+    ('s2', 3, 1, 1, 0, -1, False, True), ('m', 0, 1), ('xb', 0, 1), ('qQ', 7), ('s2', 0, 1, 0, 0, -1, False, False),
+    ('aQ', 4, 0, 2), ('aQ', 4, 2, 4), ('sg', 5, 2, 3), ('s2', 1, 0, 0, 0, -1, False, False), ('s2', 1, 1, 0, 0, -1, False, False),
+    ('mu', 5, 3), ('s1', 6, 0, 0, 2, 0), ('s1', 6, 1, 0, 2, 4), ('s1', 6, 2, 0, 2, 3), ('sg', 5, 2, 1),
+    ('s2', 2, 0, 0, 0, -1, False, False), ('xb', 1, 2), ('s1', 6, 3, 0, 2, 5), ('s2', 2, 1, 1, 1, -1, False, False), ('s2', 2, 1, 0, 0, -1, False, False),
+    ('sg', 6, 0, 2), ('mu', 5, 1), ('s2', 3, 0, 0, 0, -1, False, False), ('m', 1, 0), ('sg', 6, 1, 3),
+    ('s2', 3, 0, 1, 1, -1, False, False), ('sg', 6, 2, 0), ('sg', 6, 0, 3), ('s2', 3, 1, 0, 0, -1, False, True), ('sg', 6, 2, 3),
+    ('sg', 6, 2, 2), ('sg', 6, 3, 1), ('xb', 2, 3), ('sg', 6, 0, 1), ('sg', 6, 0, 0),
+    ('sg', 6, 1, 2), ('s2', 4, 0, 0, 1, 2, True, False), ('sg', 6, 2, 1), ('sg', 6, 3, 2), ('sg', 6, 1, 1),
+    ('mu', 5, 0), ('sg', 6, 1, 0), ('sg', 6, 3, 0), ('s1', 7, 0, 0, 2, 0), ('mu', 5, 2),
+    ('sg', 7, 0, 2), ('m', 0, 0), ('s1', 7, 1, 0, 2, 3), ('aQ', 5, 2, 4), ('aQ', 5, 0, 2),
+    ('s1', 7, 2, 0, 2, 4), ('s2', 4, 0, 0, 0, 6, True, False), ('sg', 6, 3, 3), ('mu', 6, 2), ('s1', 7, 3, 0, 2, 5),
+    ('s2', 4, 1, 0, 1, -1, False, False), ('mu', 6, 0), ('s2', 4, 2, 0, 1, -1, False, False), ('s2', 4, 3, 0, 1, -1, False, False), ('sg', 7, 2, 3),
+    ('s2', 4, 1, 0, 0, -1, False, False), ('s2', 3, 1, 1, 1, -1, False, True), ('xb', 3, 4), ('y', 0, 0, 2, 5), ('sg', 7, 3, 0),
+    ('s2', 4, 2, 0, 0, -1, False, False), ('sg', 7, 0, 1), ('s2', 4, 3, 0, 0, -1, False, False), ('s2', 5, 0, 0, 1, -1, False, False), ('s2', 5, 0, 0, 0, -1, False, False),
+    ('s2', 5, 1, 0, 1, -1, False, False), ('sg', 7, 0, 0), ('sg', 7, 1, 0), ('mu', 6, 1), ('s2', 5, 1, 0, 0, -1, False, False),
+    ('mu', 6, 3), ('m', 1, 1), ('aQ', 6, 0, 2), ('s2', 5, 2, 0, 0, -1, False, False), ('sg', 7, 1, 3),
+    ('sg', 7, 0, 3), ('aQ', 6, 2, 4), ('sg', 7, 3, 1), ('sg', 7, 2, 0), ('s2', 6, 0, 0, 0, 0, True, False),
+    ('sg', 7, 1, 2), ('s2', 6, 0, 0, 1, 1, True, False), ('sg', 7, 2, 2), ('sg', 7, 2, 1), ('sg', 7, 3, 3),
+    ('sg', 7, 3, 2), ('sg', 7, 1, 1), ('yR', 0, 0), ('mu', 7, 0), ('mu', 7, 3),
+    ('mu', 7, 2), ('s2', 6, 1, 0, 0, -1, False, False), ('s2', 6, 2, 0, 0, -1, False, False), ('y', 1, 0, 2, 6), ('s2', 5, 2, 0, 1, -1, False, False),
+    ('s2', 6, 3, 0, 0, -1, False, False), ('s2', 6, 1, 0, 1, -1, False, False), ('yR', 0, 1), ('mu', 7, 1), ('yR', 1, 1),
+    ('aQ', 7, 0, 1), ('s2', 6, 2, 0, 1, -1, False, False), ('aQ', 7, 2, 3), ('s2', 5, 3, 0, 1, -1, False, True), ('aQ', 7, 1, 2),
+    ('s2', 6, 3, 0, 1, -1, False, False), ('s2', 5, 3, 0, 0, -1, False, True), ('aQ', 7, 3, 4), ('yR', 1, 0), ('m', 2, 1),
+    ('s2', 7, 0, 0, 0, -1, False, False), ('m', 2, 0), ('s2', 7, 1, 0, 0, -1, False, False), ('yT', 1, 4), ('y', 2, 1, 2, 106),
+    ('yT', 0, 5), ('s2', 7, 2, 0, 0, -1, False, False), ('yC', 1, False), ('s2', 7, 3, 0, 0, -1, False, True), ('y', 2, 0, 1, 105),
+    ('yC', 0, False), ('m', 3, 0), ('yQ', 0), ('s2', 7, 0, 0, 1, -1, False, False), ('s2', 7, 1, 0, 1, -1, False, False),
+    ('yQ', 1), ('yR', 2, 0), ('s2', 7, 2, 0, 1, -1, False, False), ('yR', 2, 1), ('s2', 7, 3, 0, 1, -1, False, True),
+    ('y', 3, 0, 1, 108), ('yT', 2, 3), ('m', 3, 1), ('yC', 2, False), ('yR', 3, 0),
+    ('yQ', 2), ('yT', 3, 2), ('yT', 4, 6), ('yC', 3, False), ('yD', 3, 1),
+    ('yQ', 3), ('yT', 5, 4), ('yC', 4, False), ('y', 3, 1, 2, 109), ('yC', 5, True),
+    ('yQ', 4), ('yQ', 5),
 ]
 
 
@@ -119,8 +129,11 @@ def tile_sigmoid_attention_folded_output_h1_kernel(
         q_raw = {b: kept("q_raw%d" % b, [P, 2, D], BF16) for b in range(8)}
         q_codes = {b: kept("q_codes%d" % b, [P, 512], U32) for b in range(4)}
         q_scales = {b: kept("q_scales%d" % b, [P, 512], U8) for b in range(4)}
+        ls_col = kept("ls_col", [P, 8], BF16)
+        ob_col = kept("ob_col", [P, 8], BF16)
+        cols32 = kept("cols32", [P, 2, 8], F32)
         ls_rows = kept("ls_rows", [P, E], BF16)
-        ob_rows = kept("ob_rows", [P, E], BF16)
+        rows32 = [ls_rows, kept("lsb_rows", [P, E], F32)]
         x_sb = {i: kept("x_sb%d" % i, [P, 2, E], BF16) for i in range(2)}
         y_codes = kept("y_codes", [P, 2, T], U32)
         y_scales = kept("y_scales", [P, 2, T], U8)
@@ -179,10 +192,13 @@ def tile_sigmoid_attention_folded_output_h1_kernel(
                     in_=vo_scales[4 * hp:4 * hp + 4, 4 * quad:4 * quad + 4, :].rearrange("k r n -> r k n").bitcast(I32))
 
         def load_ls():
+            nc.sync.dma_start(out=ls_col[:], in_=layer_scale.rearrange("(p c) -> p c", c=8))
+
+        def load_ls_rows():
             nc.sync.dma_start(out=ls_rows[:], in_=layer_scale.partition_broadcast(P))
 
         def load_ob():
-            nc.sync.dma_start(out=ob_rows[:], in_=out_bias.partition_broadcast(P))
+            nc.sync.dma_start(out=ob_col[:], in_=out_bias.rearrange("(p c) -> p c", c=8))
 
         def permute_kt_words(g):
             cols = slice(g * 1024, (g + 1) * 1024)
@@ -323,36 +339,60 @@ def tile_sigmoid_attention_folded_output_h1_kernel(
         def engine(slot):
             return nc.vector if slot >= 100 else nc.gpsimd
 
-        def make_lsb(slot):
-            live["lsb"] = shared(slot, [P, E], F32)
-            engine(slot).tensor_tensor(out=live["lsb"][:], in0=ls_rows[:], in1=ob_rows[:], op=ALU.mult)
+        def make_cols():
+            nc.vector.tensor_tensor(out=cols32[:, 1, :], in0=ls_col[:], in1=ob_col[:], op=ALU.mult)
+
+        def spread(v, half, bk):
+            bank = bank_tile(bk, [P, 4, P], F32)
+            for c in range(4):
+                col = cols32[:, v, 4 * half + c:4 * half + c + 1]
+                nc.tensor.transpose(bank[:, c, :], col.to_broadcast([P, P]), ident_f32[:])
+            live["spread", v, half] = bank
+
+        def copy_spread(v, half, on_vector):
+            dst = rows32[v][:].rearrange("p (q c) -> p q c", c=8)[:, :, 4 * half:4 * half + 4]
+            src = live["spread", v, half][:].rearrange("p c q -> p q c")
+            if on_vector:
+                nc.vector.tensor_copy(out=dst, in_=src)
+            else:
+                nc.scalar.copy(out=dst, in_=src)
 
         def make_xb(i, slot):
             live["xb", i] = shared(slot, [P, E], F32)
             engine(slot).tensor_tensor(
-                out=live["xb", i][:], in0=x_sb[i // 2][:, i % 2, :], in1=live["lsb"][:], op=ALU.add)
+                out=live["xb", i][:], in0=x_sb[i // 2][:, i % 2, :], in1=rows32[1][:], op=ALU.add)
 
         def scale_o(i, eg):
             c, j = tiles[i]
             if ("m", i) not in live:
-                live["m", i] = work.tile([P, E], F32, name="m", bufs=2)
+                live["m", i] = work.tile([P, E], F32, name="m", bufs=4)
             cols = slice(eg * 512, (eg + 1) * 512)
             nc.vector.tensor_tensor(
                 out=live["m", i][:, cols], in0=live["acc", c, j, eg][:], in1=ls_rows[:, cols], op=ALU.mult)
 
         def finish_y(i, lo, hi, slot):
-            if ("y", i) not in live:
-                live["y", i] = shared(slot, [P, E], F32)
+            y = shared(slot, [P, (hi - lo) * 512], F32)
+            for eg in range(lo, hi):
+                live["y", i, eg] = y[:, (eg - lo) * 512:(eg - lo + 1) * 512]
             cols = slice(lo * 512, hi * 512)
             engine(slot).tensor_tensor(
-                out=live["y", i][:, cols], in0=live["m", i][:, cols], in1=live["xb", i][:, cols], op=ALU.add)
-            nc.sync.dma_start(out=out_0[i * P:(i + 1) * P, cols], in_=live["y", i][:, cols])
+                out=y[:], in0=live["m", i][:, cols], in1=live["xb", i][:, cols], op=ALU.add)
+            nc.sync.dma_start(out=out_0[i * P:(i + 1) * P, cols], in_=y[:])
 
         def round_y(i, eg):
             y16 = work.tile([P, 512], BF16, name="y16", bufs=4, align_bytes=64)
             nc.scalar.copy(
                 out=y16[:].rearrange("p (u q i) -> p u q i", u=2, i=2),
-                in_=live["y", i][:, eg * 512:(eg + 1) * 512].rearrange("p (q u i) -> p u q i", u=2, i=2))
+                in_=live["y", i, eg].rearrange("p (q u i) -> p u q i", u=2, i=2))
+            live["y16", i, eg] = y16
+
+        def round_y_direct(i, eg):
+            y16 = work.tile([P, 512], BF16, name="y16", bufs=4, align_bytes=64)
+            cols = slice(eg * 512, (eg + 1) * 512)
+            nc.vector.tensor_tensor(
+                out=y16[:].rearrange("p (u q i) -> p u q i", u=2, i=2),
+                in0=live["m", i][:, cols].rearrange("p (q u i) -> p u q i", u=2, i=2),
+                in1=live["xb", i][:, cols].rearrange("p (q u i) -> p u q i", u=2, i=2), op=ALU.add)
             live["y16", i, eg] = y16
 
         def turn_y(grp, bk):
@@ -394,10 +434,10 @@ def tile_sigmoid_attention_folded_output_h1_kernel(
 
         steps = {
             "lq": load_q, "lvo": load_vo, "lx": load_x, "lktw": load_ktw, "lkts": load_kts, "lrows": load_rows,
-            "lvos": load_vos, "lls": load_ls, "lob": load_ob,
+            "lvos": load_vos, "lls": load_ls, "lob": load_ob, "lbc": load_ls_rows,
             "pw": permute_kt_words, "ps": permute_kt_scales, "rT": turn_key_rows, "rC": take_key_rows,
             "qT": turn_q, "qC": copy_q, "qQ": quant_q, "s1": scores, "sg": sigmoid, "mu": apply_gain,
-            "aQ": quant_a, "ga": gain_rows, "il": interleave, "s2": project, "lsb": make_lsb, "xb": make_xb, "m": scale_o, "y": finish_y,
+            "aQ": quant_a, "ga": gain_rows, "il": interleave, "s2": project, "col": make_cols, "bT": spread, "bC": copy_spread, "yD": round_y_direct, "xb": make_xb, "m": scale_o, "y": finish_y,
             "yR": round_y, "yT": turn_y, "yC": copy_y, "yQ": quant_y,
         }
 

@@ -17,77 +17,78 @@ ACT = mybir.ActivationFunctionType
 ALU = mybir.AluOpType
 
 P = 128
-RUN = 2
+RUN = 4
 CHUNKS = [256, 128, 128]
+SIG_BUFS = 4
 GAIN_IN_PSUM = True
 NEED_GAIN = False
 Y_GROUPS = [[(0, 0), (1, 0)], [(0, 1), (1, 1)], [(2, 0)], [(2, 1)], [(3, 0)], [(3, 1)]]
-LOADS = [('lktw', 0, 1), ('lq', 0), ('lkts', 0), ('lrows', 0), ('lq', 1), ('lktw', 1, 2), ('lq', 2), ('lq', 3), ('lls',), ('lob',), ('lvos', 0), ('lvo', 0, 0), ('lq', 4), ('lq', 5), ('lvo', 0, 1), ('lx', 0), ('lvos', 1), ('lvo', 1, 0), ('lq', 6), ('lq', 7), ('lvo', 1, 1), ('lx', 1), ('lbc',)]
+LOADS = [('lq', 0), ('lktw', 0, 1), ('lkts', 0), ('lrows', 0), ('lq', 1), ('lktw', 1, 2), ('lqq', 1), ('lls',), ('lob',), ('lvos', 0), ('lvo', 0, 0), ('lqq', 2), ('lvo', 0, 1), ('lx', 0), ('lvos', 1), ('lvo', 1, 0), ('lqq', 3), ('lvo', 1, 1), ('lx', 1), ('lbc',)]
 ORDER = [
-    ('qT', 0, 0), ('pw', 0), ('rT', 7), ('ps', 0), ('qT', 1, 1),
-    ('ps', 1), ('qC', 0, False), ('qQ', 0), ('qC', 1, False), ('rC',),
-    ('s1', 0, 0, 0, 1, 2), ('s1', 0, 1, 0, 1, 3), ('pw', 1), ('s1', 0, 2, 0, 1, 4), ('s1', 0, 3, 0, 1, 5),
-    ('qQ', 1), ('sg', 0, 0, 0), ('qT', 2, 6), ('s1', 0, 0, 1, 2, 0), ('s1', 0, 1, 1, 2, 1),
-    ('col',), ('sg', 0, 2, 0), ('sg', 0, 3, 0), ('sg', 0, 1, 0), ('qC', 2, False),
-    ('s1', 0, 2, 1, 2, 2), ('s1', 0, 3, 1, 2, 4), ('sg', 0, 2, 1), ('sg', 0, 0, 1), ('qT', 3, 5),
-    ('s1', 1, 0, 0, 2, 3), ('s1', 1, 1, 0, 2, 6), ('mu', 0, 0), ('sg', 0, 1, 1), ('qC', 3, True),
-    ('qQ', 2), ('s1', 1, 2, 0, 2, 2), ('sg', 0, 3, 1), ('sg', 1, 0, 0), ('s1', 1, 3, 0, 2, 0),
-    ('sg', 1, 1, 1), ('sg', 1, 2, 1), ('bT', 1, 0, 1), ('qQ', 3), ('mu', 0, 1),
-    ('bT', 1, 1, 4), ('s1', 2, 0, 0, 2, 5), ('sg', 1, 1, 0), ('sg', 1, 0, 1), ('sg', 1, 2, 0),
-    ('s1', 2, 1, 0, 2, 6), ('sg', 1, 3, 0), ('qT', 5, 3), ('bC', 1, 1, False), ('qT', 4, 2),
-    ('aQ', 0, 0, 2), ('sg', 1, 3, 1), ('aQ', 0, 2, 4), ('qC', 5, False), ('s1', 2, 2, 0, 2, 4),
-    ('s2', 0, 0, 0, 1, 0, True, False), ('qC', 4, False), ('s1', 2, 3, 0, 2, 3), ('sg', 2, 2, 0), ('s2', 0, 0, 1, 0, 2, True, False),
-    ('mu', 1, 0), ('bC', 1, 0, True), ('s2', 0, 0, 1, 1, 1, True, False), ('sg', 2, 2, 1), ('s2', 0, 1, 0, 1, -1, False, False),
-    ('aQ', 1, 0, 2), ('qQ', 5), ('s1', 3, 0, 0, 2, 4), ('s2', 0, 1, 1, 1, -1, False, False), ('sg', 2, 3, 0),
-    ('sg', 2, 3, 1), ('sg', 2, 1, 0), ('mu', 1, 1), ('sg', 2, 1, 1), ('s1', 3, 1, 0, 2, 3),
-    ('sg', 2, 0, 1), ('sg', 2, 0, 0), ('s2', 1, 0, 0, 1, -1, False, False), ('sg', 3, 1, 0), ('qQ', 4),
-    ('s2', 0, 1, 1, 0, -1, False, False), ('aQ', 1, 2, 4), ('s1', 3, 2, 0, 2, 6), ('sg', 3, 0, 0), ('sg', 3, 1, 1),
-    ('s2', 1, 0, 1, 0, -1, False, False), ('s2', 1, 1, 1, 0, -1, False, False), ('mu', 2, 0), ('s1', 3, 3, 0, 2, 5), ('sg', 3, 2, 0),
-    ('mu', 2, 1), ('sg', 3, 0, 1), ('s2', 1, 0, 1, 1, -1, False, False), ('sg', 3, 3, 1), ('s2', 1, 1, 0, 1, -1, False, False),
-    ('s1', 4, 0, 0, 2, 3), ('sg', 3, 3, 0), ('sg', 3, 2, 1), ('aQ', 2, 0, 2), ('aQ', 2, 2, 4),
-    ('s1', 4, 1, 0, 2, 4), ('sg', 4, 0, 0), ('sg', 4, 1, 2), ('sg', 4, 0, 1), ('qT', 6, 5),
-    ('s1', 4, 2, 0, 2, 6), ('sg', 4, 1, 0), ('sg', 4, 0, 3), ('s2', 2, 0, 0, 1, -1, False, False), ('qC', 6, False),
-    ('s2', 2, 1, 0, 1, -1, False, False), ('s1', 4, 3, 0, 2, 5), ('sg', 4, 2, 2), ('sg', 4, 2, 0), ('sg', 4, 0, 2),
-    ('s2', 1, 1, 1, 1, -1, False, False), ('sg', 4, 2, 1), ('sg', 4, 1, 3), ('sg', 4, 1, 1), ('s2', 2, 0, 1, 0, -1, False, False),
-    ('mu', 3, 0), ('sg', 4, 3, 3), ('qT', 7, 3), ('mu', 3, 1), ('sg', 4, 2, 3),
-    ('s1', 5, 0, 0, 2, 4), ('sg', 4, 3, 2), ('sg', 4, 3, 1), ('s1', 5, 1, 0, 2, 6), ('qQ', 6),
-    ('aQ', 3, 2, 4), ('sg', 4, 3, 0), ('aQ', 3, 0, 2), ('s1', 5, 2, 0, 2, 5), ('qC', 7, False),
-    ('s2', 2, 1, 1, 0, -1, False, False), ('s2', 3, 0, 0, 1, -1, False, False), ('s2', 2, 0, 1, 1, -1, False, False), ('sg', 5, 1, 3), ('sg', 5, 1, 2),
-    ('sg', 5, 1, 1), ('mu', 4, 3), ('sg', 5, 2, 2), ('sg', 5, 2, 0), ('sg', 5, 1, 0),
-    ('s1', 5, 3, 0, 2, 3), ('sg', 5, 3, 3), ('s2', 3, 0, 1, 0, -1, False, False), ('sg', 5, 0, 0), ('mu', 4, 1),
-    ('s2', 3, 1, 0, 1, -1, False, True), ('sg', 5, 0, 1), ('mu', 4, 0), ('sg', 5, 0, 2), ('sg', 5, 3, 0),
-    ('s2', 0, 0, 0, 0, 6, True, False), ('mu', 4, 2), ('sg', 5, 3, 2), ('sg', 5, 0, 3), ('sg', 5, 3, 1),
-    ('s2', 3, 1, 1, 0, -1, False, True), ('m', 0, 1), ('xb', 0, 1), ('qQ', 7), ('s2', 0, 1, 0, 0, -1, False, False),
-    ('aQ', 4, 0, 2), ('aQ', 4, 2, 4), ('sg', 5, 2, 3), ('s2', 1, 0, 0, 0, -1, False, False), ('s2', 1, 1, 0, 0, -1, False, False),
-    ('mu', 5, 3), ('s1', 6, 0, 0, 2, 0), ('s1', 6, 1, 0, 2, 4), ('s1', 6, 2, 0, 2, 3), ('sg', 5, 2, 1),
-    ('s2', 2, 0, 0, 0, -1, False, False), ('xb', 1, 2), ('s1', 6, 3, 0, 2, 5), ('s2', 2, 1, 1, 1, -1, False, False), ('s2', 2, 1, 0, 0, -1, False, False),
-    ('sg', 6, 0, 2), ('mu', 5, 1), ('s2', 3, 0, 0, 0, -1, False, False), ('m', 1, 0), ('sg', 6, 1, 3),
-    ('s2', 3, 0, 1, 1, -1, False, False), ('sg', 6, 2, 0), ('sg', 6, 0, 3), ('s2', 3, 1, 0, 0, -1, False, True), ('sg', 6, 2, 3),
-    ('sg', 6, 2, 2), ('sg', 6, 3, 1), ('xb', 2, 3), ('sg', 6, 0, 1), ('sg', 6, 0, 0),
-    ('sg', 6, 1, 2), ('s2', 4, 0, 0, 1, 2, True, False), ('sg', 6, 2, 1), ('sg', 6, 3, 2), ('sg', 6, 1, 1),
-    ('mu', 5, 0), ('sg', 6, 1, 0), ('sg', 6, 3, 0), ('s1', 7, 0, 0, 2, 0), ('mu', 5, 2),
-    ('sg', 7, 0, 2), ('m', 0, 0), ('s1', 7, 1, 0, 2, 3), ('aQ', 5, 2, 4), ('aQ', 5, 0, 2),
-    ('s1', 7, 2, 0, 2, 4), ('s2', 4, 0, 0, 0, 6, True, False), ('sg', 6, 3, 3), ('mu', 6, 2), ('s1', 7, 3, 0, 2, 5),
-    ('s2', 4, 1, 0, 1, -1, False, False), ('mu', 6, 0), ('s2', 4, 2, 0, 1, -1, False, False), ('s2', 4, 3, 0, 1, -1, False, False), ('sg', 7, 2, 3),
-    ('s2', 4, 1, 0, 0, -1, False, False), ('s2', 3, 1, 1, 1, -1, False, True), ('xb', 3, 4), ('y', 0, 0, 2, 5), ('sg', 7, 3, 0),
-    ('s2', 4, 2, 0, 0, -1, False, False), ('sg', 7, 0, 1), ('s2', 4, 3, 0, 0, -1, False, False), ('s2', 5, 0, 0, 1, -1, False, False), ('s2', 5, 0, 0, 0, -1, False, False),
-    ('s2', 5, 1, 0, 1, -1, False, False), ('sg', 7, 0, 0), ('sg', 7, 1, 0), ('mu', 6, 1), ('s2', 5, 1, 0, 0, -1, False, False),
-    ('mu', 6, 3), ('m', 1, 1), ('aQ', 6, 0, 2), ('s2', 5, 2, 0, 0, -1, False, False), ('sg', 7, 1, 3),
-    ('sg', 7, 0, 3), ('aQ', 6, 2, 4), ('sg', 7, 3, 1), ('sg', 7, 2, 0), ('s2', 6, 0, 0, 0, 0, True, False),
-    ('sg', 7, 1, 2), ('s2', 6, 0, 0, 1, 1, True, False), ('sg', 7, 2, 2), ('sg', 7, 2, 1), ('sg', 7, 3, 3),
-    ('sg', 7, 3, 2), ('sg', 7, 1, 1), ('yR', 0, 0), ('mu', 7, 0), ('mu', 7, 3),
-    ('mu', 7, 2), ('s2', 6, 1, 0, 0, -1, False, False), ('s2', 6, 2, 0, 0, -1, False, False), ('y', 1, 0, 2, 6), ('s2', 5, 2, 0, 1, -1, False, False),
-    ('s2', 6, 3, 0, 0, -1, False, False), ('s2', 6, 1, 0, 1, -1, False, False), ('yR', 0, 1), ('mu', 7, 1), ('yR', 1, 1),
-    ('aQ', 7, 0, 1), ('s2', 6, 2, 0, 1, -1, False, False), ('aQ', 7, 2, 3), ('s2', 5, 3, 0, 1, -1, False, True), ('aQ', 7, 1, 2),
-    ('s2', 6, 3, 0, 1, -1, False, False), ('s2', 5, 3, 0, 0, -1, False, True), ('aQ', 7, 3, 4), ('yR', 1, 0), ('m', 2, 1),
-    ('s2', 7, 0, 0, 0, -1, False, False), ('m', 2, 0), ('s2', 7, 1, 0, 0, -1, False, False), ('yT', 1, 4), ('y', 2, 1, 2, 106),
-    ('yT', 0, 5), ('s2', 7, 2, 0, 0, -1, False, False), ('yC', 1, False), ('s2', 7, 3, 0, 0, -1, False, True), ('y', 2, 0, 1, 105),
-    ('yC', 0, False), ('m', 3, 0), ('yQ', 0), ('s2', 7, 0, 0, 1, -1, False, False), ('s2', 7, 1, 0, 1, -1, False, False),
-    ('yQ', 1), ('yR', 2, 0), ('s2', 7, 2, 0, 1, -1, False, False), ('yR', 2, 1), ('s2', 7, 3, 0, 1, -1, False, True),
-    ('y', 3, 0, 1, 108), ('yT', 2, 3), ('m', 3, 1), ('yC', 2, False), ('yR', 3, 0),
-    ('yQ', 2), ('yT', 3, 2), ('yT', 4, 6), ('yC', 3, False), ('yD', 3, 1),
-    ('yQ', 3), ('yT', 5, 4), ('yC', 4, False), ('y', 3, 1, 2, 109), ('yC', 5, True),
-    ('yQ', 4), ('yQ', 5),
+    ('qT', 0, 0), ('pw', 0), ('rT', 7), ('ps', 0), ('ps', 1),
+    ('qC', 0, False), ('qQ', 0), ('qT', 1, 1), ('s1', 0, 0, 0, 1, 2), ('pw', 1),
+    ('rC',), ('qC', 1, False), ('s1', 0, 1, 0, 1, 3), ('qQ', 1), ('s1', 0, 2, 0, 1, 4),
+    ('s1', 0, 3, 0, 1, 5), ('sg', 0, 1, 0), ('qT', 2, 6), ('s1', 0, 0, 1, 2, 0), ('sg', 0, 2, 0),
+    ('s1', 0, 1, 1, 2, 1), ('s1', 0, 2, 1, 2, 3), ('col',), ('qC', 2, True), ('sg', 0, 0, 0),
+    ('s1', 0, 3, 1, 2, 4), ('sg', 0, 3, 0), ('sg', 0, 0, 1), ('qT', 3, 2), ('sg', 0, 2, 1),
+    ('bT', 1, 1, 5), ('sg', 0, 1, 1), ('sg', 0, 3, 1), ('bT', 1, 0, 6), ('qC', 3, False),
+    ('s1', 1, 0, 0, 2, 0), ('mu', 0, 0), ('s1', 1, 1, 0, 2, 3), ('s1', 1, 2, 0, 2, 1), ('s1', 1, 3, 0, 2, 4),
+    ('qQ', 2), ('bC', 1, 1, True), ('qQ', 3), ('s1', 2, 0, 0, 2, 2), ('bC', 1, 0, False),
+    ('mu', 0, 1), ('aQ', 0, 0, 2), ('sg', 1, 0, 0), ('sg', 1, 0, 1), ('qT', 5, 5),
+    ('qC', 5, True), ('sg', 1, 1, 0), ('sg', 1, 1, 1), ('sg', 1, 2, 0), ('sg', 1, 2, 1),
+    ('sg', 1, 3, 0), ('sg', 1, 3, 1), ('qT', 4, 6), ('aQ', 0, 2, 4), ('qQ', 5),
+    ('sg', 2, 0, 0), ('sg', 2, 0, 1), ('s1', 2, 1, 0, 2, 0), ('qC', 4, False), ('s1', 2, 2, 0, 2, 3),
+    ('mu', 1, 0), ('s1', 2, 3, 0, 2, 1), ('sg', 2, 3, 0), ('sg', 2, 3, 1), ('s2', 0, 0, 0, 1, 5, True, False),
+    ('s2', 0, 0, 1, 1, 4, True, False), ('sg', 2, 1, 0), ('sg', 2, 1, 1), ('s2', 0, 1, 0, 1, -1, False, False), ('s2', 0, 1, 1, 1, -1, False, False),
+    ('s2', 0, 0, 0, 0, 2, True, False), ('s2', 0, 0, 1, 0, 6, True, False), ('s1', 3, 0, 0, 2, 1), ('s2', 0, 1, 0, 0, -1, False, False), ('s2', 0, 1, 1, 0, -1, False, False),
+    ('sg', 2, 2, 0), ('sg', 2, 2, 1), ('mu', 1, 1), ('s1', 3, 1, 0, 2, 0), ('xb', 0, 0),
+    ('aQ', 1, 0, 2), ('qQ', 4), ('s1', 3, 2, 0, 2, 3), ('s2', 1, 0, 0, 0, -1, False, False), ('s2', 1, 0, 1, 0, -1, False, False),
+    ('aQ', 1, 2, 4), ('sg', 3, 0, 0), ('sg', 3, 0, 1), ('sg', 3, 1, 0), ('sg', 3, 1, 1),
+    ('s1', 3, 3, 0, 2, 1), ('mu', 2, 0), ('sg', 3, 2, 0), ('sg', 3, 2, 1), ('mu', 2, 1),
+    ('s1', 4, 0, 0, 2, 0), ('s2', 1, 1, 0, 0, -1, False, False), ('s2', 1, 1, 1, 0, -1, False, False), ('s2', 1, 0, 0, 1, -1, False, False), ('s2', 1, 0, 1, 1, -1, False, False),
+    ('sg', 3, 3, 0), ('sg', 3, 3, 1), ('mu', 3, 0), ('sg', 4, 0, 0), ('sg', 4, 0, 1),
+    ('sg', 4, 0, 2), ('sg', 4, 0, 3), ('s1', 4, 1, 0, 2, 3), ('sg', 4, 1, 0), ('sg', 4, 1, 1),
+    ('sg', 4, 1, 2), ('sg', 4, 1, 3), ('qT', 6, 1), ('aQ', 2, 0, 2), ('qT', 7, 0),
+    ('s1', 4, 2, 0, 2, 3), ('qC', 6, False), ('aQ', 3, 0, 2), ('s2', 1, 1, 0, 1, -1, False, False), ('s2', 1, 1, 1, 1, -1, False, False),
+    ('s1', 4, 3, 0, 2, 1), ('qC', 7, False), ('xb', 1, 3), ('sg', 4, 2, 0), ('sg', 4, 2, 1),
+    ('sg', 4, 2, 2), ('sg', 4, 2, 3), ('mu', 3, 1), ('s1', 5, 0, 0, 2, 0), ('s2', 2, 0, 0, 0, -1, False, False),
+    ('s2', 2, 0, 1, 0, -1, False, False), ('s2', 2, 0, 0, 1, -1, False, False), ('s2', 2, 0, 1, 1, -1, False, False), ('sg', 4, 3, 0), ('sg', 4, 3, 1),
+    ('sg', 4, 3, 2), ('sg', 4, 3, 3), ('qQ', 6), ('aQ', 2, 2, 4), ('s2', 2, 1, 0, 1, -1, False, False),
+    ('s2', 2, 1, 1, 1, -1, False, False), ('qQ', 7), ('s2', 2, 1, 0, 0, -1, False, False), ('s2', 2, 1, 1, 0, -1, False, False), ('s2', 3, 0, 0, 0, -1, False, False),
+    ('s2', 3, 0, 1, 0, -1, False, False), ('aQ', 3, 2, 4), ('sg', 5, 0, 0), ('sg', 5, 0, 1), ('sg', 5, 0, 2),
+    ('sg', 5, 0, 3), ('mu', 4, 0), ('mu', 4, 1), ('mu', 4, 2), ('mu', 4, 3),
+    ('s2', 3, 1, 0, 0, -1, False, True), ('s2', 3, 1, 1, 0, -1, False, True), ('s1', 5, 1, 0, 2, 3), ('m', 0, 0), ('m', 1, 0),
+    ('aQ', 4, 0, 2), ('sg', 5, 1, 0), ('sg', 5, 1, 1), ('sg', 5, 1, 2), ('sg', 5, 1, 3),
+    ('s2', 3, 0, 0, 1, -1, False, False), ('s2', 3, 0, 1, 1, -1, False, False), ('s1', 5, 2, 0, 2, 1), ('aQ', 4, 2, 4), ('s2', 3, 1, 0, 1, -1, False, True),
+    ('s2', 3, 1, 1, 1, -1, False, True), ('s1', 5, 3, 0, 2, 0), ('sg', 5, 2, 0), ('sg', 5, 2, 1), ('sg', 5, 2, 2),
+    ('sg', 5, 2, 3), ('xb', 2, 7), ('s1', 6, 0, 0, 2, 2), ('s1', 6, 1, 0, 2, 3), ('s1', 6, 2, 0, 2, 6),
+    ('s2', 4, 0, 0, 1, 1, True, False), ('s2', 4, 1, 0, 1, 1, False, False), ('sg', 5, 3, 0), ('sg', 5, 3, 1), ('sg', 5, 3, 2),
+    ('sg', 5, 3, 3), ('s2', 4, 2, 0, 1, -1, False, False), ('s2', 4, 3, 0, 1, -1, False, False), ('s1', 6, 3, 0, 2, 0), ('sg', 6, 1, 0),
+    ('sg', 6, 1, 1), ('sg', 6, 1, 2), ('sg', 6, 1, 3), ('s1', 7, 0, 0, 2, 3), ('m', 0, 1),
+    ('sg', 6, 2, 0), ('sg', 6, 2, 1), ('sg', 6, 2, 2), ('sg', 6, 2, 3), ('s1', 7, 1, 0, 2, 5),
+    ('m', 1, 1), ('mu', 5, 2), ('mu', 5, 3), ('mu', 5, 0), ('mu', 5, 1),
+    ('sg', 6, 0, 0), ('sg', 6, 0, 1), ('sg', 6, 0, 2), ('sg', 6, 0, 3), ('aQ', 5, 2, 4),
+    ('sg', 6, 3, 0), ('sg', 6, 3, 1), ('sg', 6, 3, 2), ('sg', 6, 3, 3), ('sg', 7, 0, 0),
+    ('sg', 7, 0, 1), ('sg', 7, 0, 2), ('sg', 7, 0, 3), ('s1', 7, 2, 0, 2, 4), ('aQ', 5, 0, 2),
+    ('s2', 4, 0, 0, 0, 6, True, False), ('s2', 4, 1, 0, 0, 6, False, False), ('y', 0, 0, 2, 6), ('sg', 7, 2, 0), ('sg', 7, 2, 1),
+    ('sg', 7, 2, 2), ('sg', 7, 2, 3), ('s1', 7, 3, 0, 2, 2), ('s2', 4, 2, 0, 0, -1, False, False), ('s2', 4, 3, 0, 0, -1, False, False),
+    ('s2', 5, 0, 0, 0, -1, False, False), ('s2', 5, 1, 0, 0, -1, False, False), ('sg', 7, 3, 0), ('sg', 7, 3, 1), ('sg', 7, 3, 2),
+    ('sg', 7, 3, 3), ('y', 1, 0, 2, 10), ('mu', 6, 0), ('mu', 6, 1), ('sg', 7, 1, 0),
+    ('sg', 7, 1, 1), ('sg', 7, 1, 2), ('sg', 7, 1, 3), ('yR', 1, 1), ('s2', 5, 2, 0, 0, -1, False, False),
+    ('s2', 5, 3, 0, 0, -1, False, True), ('s2', 5, 0, 0, 1, -1, False, False), ('s2', 5, 1, 0, 1, -1, False, False), ('mu', 6, 2), ('mu', 6, 3),
+    ('s2', 5, 2, 0, 1, -1, False, False), ('s2', 5, 3, 0, 1, -1, False, True), ('m', 2, 0), ('aQ', 6, 2, 4), ('aQ', 6, 0, 2),
+    ('mu', 7, 3), ('yR', 1, 0), ('s2', 6, 0, 0, 1, 0, True, False), ('s2', 6, 1, 0, 1, 0, False, False), ('mu', 7, 2),
+    ('s2', 6, 2, 0, 1, -1, False, False), ('s2', 6, 3, 0, 1, -1, False, False), ('yR', 0, 1), ('mu', 7, 0), ('mu', 7, 1),
+    ('s2', 6, 0, 0, 0, 3, True, False), ('s2', 6, 1, 0, 0, 3, False, False), ('m', 2, 1), ('xb', 3, 12), ('yT', 1, 4),
+    ('yR', 0, 0), ('yT', 0, 2), ('s2', 6, 2, 0, 0, -1, False, False), ('s2', 6, 3, 0, 0, -1, False, False), ('aQ', 7, 0, 2),
+    ('aQ', 7, 2, 3), ('s2', 7, 0, 0, 0, -1, False, False), ('s2', 7, 1, 0, 0, -1, False, False), ('s2', 7, 2, 0, 0, -1, False, False), ('y', 2, 0, 1, 292),
+    ('aQ', 7, 3, 4), ('s2', 7, 3, 0, 0, -1, False, True), ('s2', 7, 0, 0, 1, -1, False, False), ('s2', 7, 1, 0, 1, -1, False, False), ('s2', 7, 2, 0, 1, -1, False, False),
+    ('yC', 0, False), ('yQ', 0), ('yR', 2, 0), ('yC', 1, False), ('s2', 7, 3, 0, 1, -1, False, True),
+    ('y', 2, 1, 2, 293), ('m', 3, 0), ('yQ', 1), ('yR', 2, 1), ('y', 3, 0, 1, 297),
+    ('m', 3, 1), ('yT', 2, 5), ('yT', 3, 6), ('yC', 2, False), ('yR', 3, 0),
+    ('yQ', 2), ('yD', 3, 1), ('yC', 3, False), ('yQ', 3), ('yT', 4, 1),
+    ('y', 3, 1, 2, 298), ('yT', 5, 2), ('yC', 5, True), ('yC', 4, False), ('yQ', 4),
+    ('yQ', 5),
 ]
 
 
@@ -116,7 +117,6 @@ def tile_sigmoid_attention_folded_output_h1_kernel(
         warm_in = kept("warm_in", [P, 8], F32)
         warm_out = kept("warm_out", [P, 8], F32)
         ident_f32 = kept("ident_f32", [P, P], F32)
-        ident_bf16 = kept("ident_bf16", [P, P], BF16)
         ktw_raw = kept("ktw_raw", [P, 2 * S], U8)
         kts_raw = kept("kts_raw", [P, S], U8)
         ktw = kept("ktw", [P, 2 * S], U8)
@@ -126,19 +126,20 @@ def tile_sigmoid_attention_folded_output_h1_kernel(
         gain = kept("gain", [P, 8, 4 * RUN], F32)
         vos = kept("vos", [P, 8, E], U8)
         vow = {(hp, g): kept("vow%d%d" % (hp, g), [P, 2, 2 * E], U8) for hp in range(2) for g in range(2)}
-        q_raw = {b: kept("q_raw%d" % b, [P, 2, D], BF16) for b in range(8)}
+        q_pair = {b: kept("q_raw%d" % b, [P, 2, 2, D], BF16) for b in range(4)}
+        q_raw = {b: q_pair[b // 2][:, b % 2] for b in range(8)}
         q_codes = {b: kept("q_codes%d" % b, [P, 512], U32) for b in range(4)}
         q_scales = {b: kept("q_scales%d" % b, [P, 512], U8) for b in range(4)}
         ls_col = kept("ls_col", [P, 8], BF16)
         ob_col = kept("ob_col", [P, 8], BF16)
         cols32 = kept("cols32", [P, 2, 8], F32)
         ls_rows = kept("ls_rows", [P, E], BF16)
+        ob_rows = kept("ob_rows", [P, E], BF16)
         rows32 = [ls_rows, kept("lsb_rows", [P, E], F32)]
+        live = {"lsb": rows32[1]}
         x_sb = {i: kept("x_sb%d" % i, [P, 2, E], BF16) for i in range(2)}
         y_codes = kept("y_codes", [P, 2, T], U32)
         y_scales = kept("y_scales", [P, 2, T], U8)
-
-        live = {}
 
         def bank_tile(b, shape, dtype):
             return psum.tile(shape, dtype, name="bank", tag="bank%d" % b)
@@ -158,7 +159,18 @@ def tile_sigmoid_attention_folded_output_h1_kernel(
                 src = queries[2 * hg + half, rows, :].rearrange("(p n) d -> p n d", n=2)
             else:
                 src = queries[2 * half:2 * half + 2, rows, :].rearrange("n p d -> p n d")
-            nc.sync.dma_start(out=q_raw[b][:], in_=src)
+            nc.sync.dma_start(out=q_raw[b], in_=src)
+
+        def load_q_pair(b):
+            c, hg, half = q_block(2 * b)
+            rows = slice(starts[c], starts[c] + CHUNKS[c])
+            if CHUNKS[c] == 256:
+                src = queries[2 * hg:2 * hg + 2, rows, :].rearrange("h (p n) d -> p h (n d)", n=2)
+                dst = q_pair[b][:].rearrange("p h n d -> p h (n d)")
+            else:
+                src = queries[:, rows, :].rearrange("h p d -> p h d")
+                dst = q_pair[b][:].rearrange("p h n d -> p (h n) d")
+            nc.sync.dma_start(out=dst, in_=src)
 
         def load_vo(hp, g):
             nc.sync.dma_start(
@@ -197,6 +209,9 @@ def tile_sigmoid_attention_folded_output_h1_kernel(
         def load_ls_rows():
             nc.sync.dma_start(out=ls_rows[:], in_=layer_scale.partition_broadcast(P))
 
+        def load_ob_rows():
+            nc.sync.dma_start(out=ob_rows[:], in_=out_bias.partition_broadcast(P))
+
         def load_ob():
             nc.sync.dma_start(out=ob_col[:], in_=out_bias.rearrange("(p c) -> p c", c=8))
 
@@ -213,22 +228,23 @@ def tile_sigmoid_attention_folded_output_h1_kernel(
                 in_=kts_raw[:, cols].rearrange("p (m t) -> p t m", t=4))
 
         def turn_key_rows(bk):
-            bank = bank_tile(bk, [P, 4, P], BF16)
-            for t in range(4):
-                nc.tensor.transpose(bank[:, t, :], key_rows[:, t:512:4], ident_bf16[:])
-            live["rows"] = bank
+            bank = bank_tile(bk, [P, 2 * P], F32)
+            words = key_rows[:].bitcast(F32)
+            for u in range(2):
+                nc.tensor.transpose(bank[:, u:2 * P:2], words[:, u:256:2], ident_f32[:])
+            live["rows"] = bank[:].bitcast(BF16).rearrange("p (r t) -> p r t", t=4)
 
         def take_key_rows():
             bank = live["rows"]
-            nc.vector.tensor_copy(out=bias[:], in_=bank[:, :, 0:8].rearrange("p t r -> p r t"))
+            nc.vector.tensor_copy(out=bias[:], in_=bank[:, 0:8, :])
             if NEED_GAIN:
                 nc.vector.tensor_copy(
                     out=gain[:].rearrange("p r (t i) -> p r t i", i=RUN),
-                    in_=bank[:, :, 8:16].rearrange("p t r -> p r t").unsqueeze(3).to_broadcast([P, 8, 4, RUN]))
+                    in_=bank[:, 8:16, :].unsqueeze(3).to_broadcast([P, 8, 4, RUN]))
 
         def turn_q(b, bk):
             bank = bank_tile(bk, [P, 4, P], F32)
-            words = q_raw[b][:].bitcast(F32)
+            words = q_raw[b].bitcast(F32)
             for n in range(2):
                 for u in range(2):
                     nc.tensor.transpose(bank[:, 2 * n + u, :], words[:, n, u:256:2], ident_f32[:])
@@ -275,22 +291,26 @@ def tile_sigmoid_attention_folded_output_h1_kernel(
         def sigmoid(k, t, hh):
             n = CHUNKS[units[k][0]]
             if ("sig", k) not in live:
-                live["sig", k] = work.tile([P, 512 // n, 4, n], F32, name="sig", bufs=3)
+                live["sig", k] = work.tile([P, 512 // n, 4, n], F32, name="sig", bufs=SIG_BUFS)
             nc.scalar.activation(
                 out=live["sig", k][:, hh, t, :], in_=live["s", k, t, hh * n // 256][:, hh * n:(hh + 1) * n],
                 func=ACT.Sigmoid, bias=bias[:, pass_of(k, hh), t:t + 1])
 
+        def a_cols(k, lo, hi):
+            half = lo // 1024
+            if ("a", k, half) not in live:
+                live["a", k, half] = shared(2 * k + half, [P, 1024], BF16)
+            return live["a", k, half][:, lo - half * 1024:hi - half * 1024]
+
         def apply_gain(k, hh):
             n = CHUNKS[units[k][0]]
             row = pass_of(k, hh)
-            if ("a", k) not in live:
-                live["a", k] = shared(k, [P, 2048], BF16)
             if GAIN_IN_PSUM:
-                gains = live["rows"][:, :, 8 + row:9 + row].unsqueeze(1)
+                gains = live["rows"][:, 8 + row, :].unsqueeze(1).unsqueeze(3)
             else:
                 gains = gain[:, row, :].rearrange("p (t i) -> p t i", i=RUN).unsqueeze(1)
             nc.vector.tensor_tensor(
-                out=live["a", k][:, hh * 4 * n:(hh + 1) * 4 * n].rearrange("p (c i t) -> p c t i", i=RUN, t=4),
+                out=a_cols(k, hh * 4 * n, (hh + 1) * 4 * n).rearrange("p (c i t) -> p c t i", i=RUN, t=4),
                 in0=live["sig", k][:, hh].rearrange("p t (c i) -> p c t i", i=RUN),
                 in1=gains.to_broadcast([P, n // RUN, 4, RUN]),
                 op=ALU.mult)
@@ -305,10 +325,8 @@ def tile_sigmoid_attention_folded_output_h1_kernel(
 
         def interleave(k, hh):
             n = CHUNKS[units[k][0]]
-            if ("a", k) not in live:
-                live["a", k] = shared(k, [P, 2048], BF16)
             nc.vector.tensor_copy(
-                out=live["a", k][:, hh * 4 * n:(hh + 1) * 4 * n].rearrange("p (c i t) -> p c t i", i=4, t=4),
+                out=a_cols(k, hh * 4 * n, (hh + 1) * 4 * n).rearrange("p (c i t) -> p c t i", i=4, t=4),
                 in_=live["ar", k, hh][:].rearrange("p t (c i) -> p c t i", i=4))
 
         def quant_a(k, lo, hi):
@@ -319,7 +337,7 @@ def tile_sigmoid_attention_folded_output_h1_kernel(
             codes, scales = live["aq", k]
             nc.vector.quantize_mx(
                 out=codes[:, lo * P:hi * P].bitcast(FP8X4), scales=scales[:, lo * P:hi * P],
-                in_=live["a", k][:, lo * 512:hi * 512])
+                in_=a_cols(k, lo * 512, hi * 512))
 
         def project(k, hh, j, eg, bk, first, last):
             c, hg, g = units[k]
@@ -338,6 +356,10 @@ def tile_sigmoid_attention_folded_output_h1_kernel(
 
         def engine(slot):
             return nc.vector if slot >= 100 else nc.gpsimd
+
+        def make_lsb(slot):
+            live["lsb"] = shared(slot, [P, E], F32)
+            engine(slot).tensor_tensor(out=live["lsb"][:], in0=ls_rows[:], in1=ob_rows[:], op=ALU.mult)
 
         def make_cols():
             nc.vector.tensor_tensor(out=cols32[:, 1, :], in0=ls_col[:], in1=ob_col[:], op=ALU.mult)
@@ -360,7 +382,7 @@ def tile_sigmoid_attention_folded_output_h1_kernel(
         def make_xb(i, slot):
             live["xb", i] = shared(slot, [P, E], F32)
             engine(slot).tensor_tensor(
-                out=live["xb", i][:], in0=x_sb[i // 2][:, i % 2, :], in1=rows32[1][:], op=ALU.add)
+                out=live["xb", i][:], in0=x_sb[i // 2][:, i % 2, :], in1=live["lsb"][:], op=ALU.add)
 
         def scale_o(i, eg):
             c, j = tiles[i]
@@ -433,7 +455,7 @@ def tile_sigmoid_attention_folded_output_h1_kernel(
                     in_=y_scales[32 * quad:32 * quad + 4, :, :].bitcast(I32))
 
         steps = {
-            "lq": load_q, "lvo": load_vo, "lx": load_x, "lktw": load_ktw, "lkts": load_kts, "lrows": load_rows,
+            "lq": load_q, "lqq": load_q_pair, "lbo": load_ob_rows, "lsb": make_lsb, "lvo": load_vo, "lx": load_x, "lktw": load_ktw, "lkts": load_kts, "lrows": load_rows,
             "lvos": load_vos, "lls": load_ls, "lob": load_ob, "lbc": load_ls_rows,
             "pw": permute_kt_words, "ps": permute_kt_scales, "rT": turn_key_rows, "rC": take_key_rows,
             "qT": turn_q, "qC": copy_q, "qQ": quant_q, "s1": scores, "sg": sigmoid, "mu": apply_gain,
@@ -446,7 +468,6 @@ def tile_sigmoid_attention_folded_output_h1_kernel(
         nc.vector.memset(warm_in[:], 0.0)
         nc.vector.memset(vos[:].rearrange("p k n -> p (k n)").bitcast(I32), 0)
         make_identity(nc, ident_f32[:])
-        make_identity(nc, ident_bf16[:])
         for step in LOADS:
             steps[step[0]](*step[1:])
         nc.scalar.activation(out=warm_out[:], in_=warm_in[:], func=ACT.Sigmoid)

@@ -23,71 +23,71 @@ SIG_BUFS = 4
 GAIN_IN_PSUM = True
 NEED_GAIN = False
 Y_GROUPS = [[(0, 0), (1, 0)], [(0, 1), (1, 1)], [(2, 0)], [(2, 1)], [(3, 0)], [(3, 1)]]
-LOADS = [('lq', 0), ('lktw', 0, 1), ('lkts', 0), ('lrows', 0), ('lq', 1), ('lktw', 1, 2), ('lqq', 1), ('lls',), ('lob',), ('lvos', 0), ('lvo', 0, 0), ('lqq', 2), ('lvo', 0, 1), ('lx', 0), ('lvos', 1), ('lvo', 1, 0), ('lqq', 3), ('lvo', 1, 1), ('lx', 1), ('lbc',)]
+LOADS = [('lq', 0), ('lktw', 0, 2), ('lq', 1), ('lkts', 0), ('lrows', 0), ('lqq', 1), ('lls',), ('lob',), ('lqq', 2), ('lvos', 0), ('lvo', 0, 0), ('lvo', 0, 1), ('lx', 0), ('lqq', 3), ('lvos', 1), ('lvo', 1, 0), ('lvo', 1, 1), ('lx', 1), ('lbc',)]
 ORDER = [
-    ('qT', 0, 0), ('pw', 0), ('rT', 7), ('ps', 0), ('ps', 1),
-    ('qC', 0, False), ('qQ', 0), ('qT', 1, 1), ('s1', 0, 0, 0, 1, 2), ('pw', 1),
-    ('rC',), ('qC', 1, False), ('s1', 0, 1, 0, 1, 3), ('qQ', 1), ('s1', 0, 2, 0, 1, 4),
-    ('s1', 0, 3, 0, 1, 5), ('sg', 0, 1, 0), ('qT', 2, 6), ('s1', 0, 0, 1, 2, 0), ('sg', 0, 2, 0),
-    ('s1', 0, 1, 1, 2, 1), ('s1', 0, 2, 1, 2, 3), ('col',), ('qC', 2, True), ('sg', 0, 0, 0),
-    ('s1', 0, 3, 1, 2, 4), ('sg', 0, 3, 0), ('sg', 0, 0, 1), ('qT', 3, 2), ('sg', 0, 2, 1),
-    ('bT', 1, 1, 5), ('sg', 0, 1, 1), ('sg', 0, 3, 1), ('bT', 1, 0, 6), ('qC', 3, False),
-    ('s1', 1, 0, 0, 2, 0), ('mu', 0, 0), ('s1', 1, 1, 0, 2, 3), ('s1', 1, 2, 0, 2, 1), ('s1', 1, 3, 0, 2, 4),
-    ('qQ', 2), ('bC', 1, 1, True), ('qQ', 3), ('s1', 2, 0, 0, 2, 2), ('bC', 1, 0, False),
-    ('mu', 0, 1), ('aQ', 0, 0, 2), ('sg', 1, 0, 0), ('sg', 1, 0, 1), ('qT', 5, 5),
-    ('qC', 5, True), ('sg', 1, 1, 0), ('sg', 1, 1, 1), ('sg', 1, 2, 0), ('sg', 1, 2, 1),
-    ('sg', 1, 3, 0), ('sg', 1, 3, 1), ('qT', 4, 6), ('aQ', 0, 2, 4), ('qQ', 5),
-    ('sg', 2, 0, 0), ('sg', 2, 0, 1), ('s1', 2, 1, 0, 2, 0), ('qC', 4, False), ('s1', 2, 2, 0, 2, 3),
-    ('mu', 1, 0), ('s1', 2, 3, 0, 2, 1), ('sg', 2, 3, 0), ('sg', 2, 3, 1), ('s2', 0, 0, 0, 1, 5, True, False),
-    ('s2', 0, 0, 1, 1, 4, True, False), ('sg', 2, 1, 0), ('sg', 2, 1, 1), ('s2', 0, 1, 0, 1, -1, False, False), ('s2', 0, 1, 1, 1, -1, False, False),
-    ('s2', 0, 0, 0, 0, 2, True, False), ('s2', 0, 0, 1, 0, 6, True, False), ('s1', 3, 0, 0, 2, 1), ('s2', 0, 1, 0, 0, -1, False, False), ('s2', 0, 1, 1, 0, -1, False, False),
-    ('sg', 2, 2, 0), ('sg', 2, 2, 1), ('mu', 1, 1), ('s1', 3, 1, 0, 2, 0), ('xb', 0, 0),
-    ('aQ', 1, 0, 2), ('qQ', 4), ('s1', 3, 2, 0, 2, 3), ('s2', 1, 0, 0, 0, -1, False, False), ('s2', 1, 0, 1, 0, -1, False, False),
-    ('aQ', 1, 2, 4), ('sg', 3, 0, 0), ('sg', 3, 0, 1), ('sg', 3, 1, 0), ('sg', 3, 1, 1),
-    ('s1', 3, 3, 0, 2, 1), ('mu', 2, 0), ('sg', 3, 2, 0), ('sg', 3, 2, 1), ('mu', 2, 1),
-    ('s1', 4, 0, 0, 2, 0), ('s2', 1, 1, 0, 0, -1, False, False), ('s2', 1, 1, 1, 0, -1, False, False), ('s2', 1, 0, 0, 1, -1, False, False), ('s2', 1, 0, 1, 1, -1, False, False),
-    ('sg', 3, 3, 0), ('sg', 3, 3, 1), ('mu', 3, 0), ('sg', 4, 0, 0), ('sg', 4, 0, 1),
-    ('sg', 4, 0, 2), ('sg', 4, 0, 3), ('s1', 4, 1, 0, 2, 3), ('sg', 4, 1, 0), ('sg', 4, 1, 1),
-    ('sg', 4, 1, 2), ('sg', 4, 1, 3), ('qT', 6, 1), ('aQ', 2, 0, 2), ('qT', 7, 0),
-    ('s1', 4, 2, 0, 2, 3), ('qC', 6, False), ('aQ', 3, 0, 2), ('s2', 1, 1, 0, 1, -1, False, False), ('s2', 1, 1, 1, 1, -1, False, False),
-    ('s1', 4, 3, 0, 2, 1), ('qC', 7, False), ('xb', 1, 3), ('sg', 4, 2, 0), ('sg', 4, 2, 1),
-    ('sg', 4, 2, 2), ('sg', 4, 2, 3), ('mu', 3, 1), ('s1', 5, 0, 0, 2, 0), ('s2', 2, 0, 0, 0, -1, False, False),
-    ('s2', 2, 0, 1, 0, -1, False, False), ('s2', 2, 0, 0, 1, -1, False, False), ('s2', 2, 0, 1, 1, -1, False, False), ('sg', 4, 3, 0), ('sg', 4, 3, 1),
-    ('sg', 4, 3, 2), ('sg', 4, 3, 3), ('qQ', 6), ('aQ', 2, 2, 4), ('s2', 2, 1, 0, 1, -1, False, False),
-    ('s2', 2, 1, 1, 1, -1, False, False), ('qQ', 7), ('s2', 2, 1, 0, 0, -1, False, False), ('s2', 2, 1, 1, 0, -1, False, False), ('s2', 3, 0, 0, 0, -1, False, False),
-    ('s2', 3, 0, 1, 0, -1, False, False), ('aQ', 3, 2, 4), ('sg', 5, 0, 0), ('sg', 5, 0, 1), ('sg', 5, 0, 2),
-    ('sg', 5, 0, 3), ('mu', 4, 0), ('mu', 4, 1), ('mu', 4, 2), ('mu', 4, 3),
-    ('s2', 3, 1, 0, 0, -1, False, True), ('s2', 3, 1, 1, 0, -1, False, True), ('s1', 5, 1, 0, 2, 3), ('m', 0, 0), ('m', 1, 0),
-    ('aQ', 4, 0, 2), ('sg', 5, 1, 0), ('sg', 5, 1, 1), ('sg', 5, 1, 2), ('sg', 5, 1, 3),
-    ('s2', 3, 0, 0, 1, -1, False, False), ('s2', 3, 0, 1, 1, -1, False, False), ('s1', 5, 2, 0, 2, 1), ('aQ', 4, 2, 4), ('s2', 3, 1, 0, 1, -1, False, True),
-    ('s2', 3, 1, 1, 1, -1, False, True), ('s1', 5, 3, 0, 2, 0), ('sg', 5, 2, 0), ('sg', 5, 2, 1), ('sg', 5, 2, 2),
-    ('sg', 5, 2, 3), ('xb', 2, 7), ('s1', 6, 0, 0, 2, 2), ('s1', 6, 1, 0, 2, 3), ('s1', 6, 2, 0, 2, 6),
-    ('s2', 4, 0, 0, 1, 1, True, False), ('s2', 4, 1, 0, 1, 1, False, False), ('sg', 5, 3, 0), ('sg', 5, 3, 1), ('sg', 5, 3, 2),
-    ('sg', 5, 3, 3), ('s2', 4, 2, 0, 1, -1, False, False), ('s2', 4, 3, 0, 1, -1, False, False), ('s1', 6, 3, 0, 2, 0), ('sg', 6, 1, 0),
-    ('sg', 6, 1, 1), ('sg', 6, 1, 2), ('sg', 6, 1, 3), ('s1', 7, 0, 0, 2, 3), ('m', 0, 1),
-    ('sg', 6, 2, 0), ('sg', 6, 2, 1), ('sg', 6, 2, 2), ('sg', 6, 2, 3), ('s1', 7, 1, 0, 2, 5),
-    ('m', 1, 1), ('mu', 5, 2), ('mu', 5, 3), ('mu', 5, 0), ('mu', 5, 1),
-    ('sg', 6, 0, 0), ('sg', 6, 0, 1), ('sg', 6, 0, 2), ('sg', 6, 0, 3), ('aQ', 5, 2, 4),
-    ('sg', 6, 3, 0), ('sg', 6, 3, 1), ('sg', 6, 3, 2), ('sg', 6, 3, 3), ('sg', 7, 0, 0),
-    ('sg', 7, 0, 1), ('sg', 7, 0, 2), ('sg', 7, 0, 3), ('s1', 7, 2, 0, 2, 4), ('aQ', 5, 0, 2),
-    ('s2', 4, 0, 0, 0, 6, True, False), ('s2', 4, 1, 0, 0, 6, False, False), ('y', 0, 0, 2, 6), ('sg', 7, 2, 0), ('sg', 7, 2, 1),
-    ('sg', 7, 2, 2), ('sg', 7, 2, 3), ('s1', 7, 3, 0, 2, 2), ('s2', 4, 2, 0, 0, -1, False, False), ('s2', 4, 3, 0, 0, -1, False, False),
-    ('s2', 5, 0, 0, 0, -1, False, False), ('s2', 5, 1, 0, 0, -1, False, False), ('sg', 7, 3, 0), ('sg', 7, 3, 1), ('sg', 7, 3, 2),
-    ('sg', 7, 3, 3), ('y', 1, 0, 2, 10), ('mu', 6, 0), ('mu', 6, 1), ('sg', 7, 1, 0),
-    ('sg', 7, 1, 1), ('sg', 7, 1, 2), ('sg', 7, 1, 3), ('yR', 1, 1), ('s2', 5, 2, 0, 0, -1, False, False),
-    ('s2', 5, 3, 0, 0, -1, False, True), ('s2', 5, 0, 0, 1, -1, False, False), ('s2', 5, 1, 0, 1, -1, False, False), ('mu', 6, 2), ('mu', 6, 3),
-    ('s2', 5, 2, 0, 1, -1, False, False), ('s2', 5, 3, 0, 1, -1, False, True), ('m', 2, 0), ('aQ', 6, 2, 4), ('aQ', 6, 0, 2),
-    ('mu', 7, 3), ('yR', 1, 0), ('s2', 6, 0, 0, 1, 0, True, False), ('s2', 6, 1, 0, 1, 0, False, False), ('mu', 7, 2),
-    ('s2', 6, 2, 0, 1, -1, False, False), ('s2', 6, 3, 0, 1, -1, False, False), ('yR', 0, 1), ('mu', 7, 0), ('mu', 7, 1),
-    ('s2', 6, 0, 0, 0, 3, True, False), ('s2', 6, 1, 0, 0, 3, False, False), ('m', 2, 1), ('xb', 3, 12), ('yT', 1, 4),
-    ('yR', 0, 0), ('yT', 0, 2), ('s2', 6, 2, 0, 0, -1, False, False), ('s2', 6, 3, 0, 0, -1, False, False), ('aQ', 7, 0, 2),
-    ('aQ', 7, 2, 3), ('s2', 7, 0, 0, 0, -1, False, False), ('s2', 7, 1, 0, 0, -1, False, False), ('s2', 7, 2, 0, 0, -1, False, False), ('y', 2, 0, 1, 292),
-    ('aQ', 7, 3, 4), ('s2', 7, 3, 0, 0, -1, False, True), ('s2', 7, 0, 0, 1, -1, False, False), ('s2', 7, 1, 0, 1, -1, False, False), ('s2', 7, 2, 0, 1, -1, False, False),
-    ('yC', 0, False), ('yQ', 0), ('yR', 2, 0), ('yC', 1, False), ('s2', 7, 3, 0, 1, -1, False, True),
-    ('y', 2, 1, 2, 293), ('m', 3, 0), ('yQ', 1), ('yR', 2, 1), ('y', 3, 0, 1, 297),
-    ('m', 3, 1), ('yT', 2, 5), ('yT', 3, 6), ('yC', 2, False), ('yR', 3, 0),
-    ('yQ', 2), ('yD', 3, 1), ('yC', 3, False), ('yQ', 3), ('yT', 4, 1),
-    ('y', 3, 1, 2, 298), ('yT', 5, 2), ('yC', 5, True), ('yC', 4, False), ('yQ', 4),
+    ('qT', 0, 0), ('pw', 0), ('qT', 1, 1), ('qC', 0, False), ('rT', 7),
+    ('ps', 0), ('qQ', 0), ('s1', 0, 0, 0, 1, 2), ('s1', 0, 1, 0, 1, 3), ('s1', 0, 2, 0, 1, 4),
+    ('qC', 1, False), ('rC',), ('s1', 0, 3, 0, 1, 5), ('qQ', 1), ('pw', 1),
+    ('s1', 0, 0, 1, 2, 6), ('s1', 0, 1, 1, 2, 0), ('s1', 0, 2, 1, 2, 1), ('sg', 0, 0, 0), ('qT', 2, 2),
+    ('sg', 0, 1, 0), ('sg', 0, 2, 0), ('sg', 0, 3, 0), ('col',), ('sg', 0, 0, 1),
+    ('sg', 0, 1, 1), ('qT', 3, 3), ('s1', 0, 3, 1, 2, 4), ('sg', 0, 2, 1), ('ps', 1),
+    ('mu', 0, 0), ('s1', 1, 0, 0, 2, 5), ('s1', 1, 1, 0, 2, 6), ('s1', 1, 2, 0, 2, 0), ('qC', 3, True),
+    ('qC', 2, False), ('sg', 0, 3, 1), ('s1', 1, 3, 0, 2, 1), ('sg', 1, 0, 0), ('sg', 1, 0, 1),
+    ('bT', 1, 0, 2), ('aQ', 0, 0, 2), ('qT', 4, 4), ('qQ', 3), ('qQ', 2),
+    ('sg', 1, 1, 0), ('sg', 1, 1, 1), ('mu', 0, 1), ('sg', 1, 2, 0), ('sg', 1, 2, 1),
+    ('sg', 1, 3, 0), ('sg', 1, 3, 1), ('s1', 2, 0, 0, 2, 3), ('s2', 0, 0, 0, 1, 5, True, False), ('s2', 0, 0, 1, 1, 6, True, False),
+    ('s1', 2, 1, 0, 2, 0), ('qT', 5, 1), ('qC', 4, False), ('sg', 2, 0, 0), ('sg', 2, 0, 1),
+    ('sg', 2, 1, 0), ('sg', 2, 1, 1), ('bC', 1, 0, True), ('bT', 1, 1, 2), ('mu', 1, 0),
+    ('aQ', 0, 2, 4), ('mu', 1, 1), ('s1', 2, 2, 0, 2, 4), ('aQ', 1, 0, 2), ('qQ', 4),
+    ('s1', 2, 3, 0, 2, 3), ('qC', 5, False), ('bC', 1, 1, False), ('qQ', 5), ('sg', 2, 2, 0),
+    ('sg', 2, 2, 1), ('sg', 2, 3, 0), ('sg', 2, 3, 1), ('s2', 0, 1, 0, 1, -1, False, False), ('s2', 0, 1, 1, 1, -1, False, False),
+    ('s1', 3, 0, 0, 2, 0), ('aQ', 1, 2, 4), ('s1', 3, 1, 0, 2, 1), ('qT', 6, 2), ('qT', 7, 4),
+    ('qC', 6, False), ('s1', 3, 2, 0, 2, 3), ('s2', 1, 0, 0, 1, -1, False, False), ('s2', 1, 0, 1, 1, -1, False, False), ('mu', 2, 0),
+    ('sg', 3, 0, 0), ('sg', 3, 0, 1), ('s1', 3, 3, 0, 2, 2), ('sg', 3, 1, 0), ('sg', 3, 1, 1),
+    ('xb', 0, 3), ('sg', 3, 2, 0), ('sg', 3, 2, 1), ('s2', 1, 1, 0, 1, -1, False, False), ('s2', 1, 1, 1, 1, -1, False, False),
+    ('s2', 0, 0, 0, 0, 0, True, False), ('s2', 0, 0, 1, 0, 1, True, False), ('mu', 2, 1), ('aQ', 2, 0, 2), ('aQ', 2, 2, 4),
+    ('sg', 3, 3, 0), ('sg', 3, 3, 1), ('mu', 3, 1), ('s2', 0, 1, 0, 0, -1, False, False), ('s2', 0, 1, 1, 0, -1, False, False),
+    ('mu', 3, 0), ('s1', 4, 0, 0, 2, 3), ('s2', 2, 0, 0, 1, -1, False, False), ('s2', 2, 0, 1, 1, -1, False, False), ('qC', 7, False),
+    ('s1', 4, 1, 0, 2, 2), ('sg', 4, 0, 0), ('sg', 4, 0, 1), ('sg', 4, 0, 2), ('sg', 4, 0, 3),
+    ('s1', 4, 2, 0, 2, 4), ('s2', 2, 1, 0, 1, -1, False, False), ('s2', 2, 1, 1, 1, -1, False, False), ('s1', 4, 3, 0, 2, 3), ('sg', 4, 1, 0),
+    ('sg', 4, 1, 1), ('sg', 4, 1, 2), ('sg', 4, 1, 3), ('sg', 4, 2, 0), ('sg', 4, 2, 1),
+    ('sg', 4, 2, 2), ('sg', 4, 2, 3), ('sg', 4, 3, 0), ('sg', 4, 3, 1), ('sg', 4, 3, 2),
+    ('sg', 4, 3, 3), ('s2', 1, 0, 0, 0, -1, False, False), ('s2', 1, 0, 1, 0, -1, False, False), ('s1', 5, 0, 0, 2, 2), ('aQ', 3, 0, 2),
+    ('s2', 1, 1, 0, 0, -1, False, False), ('s2', 1, 1, 1, 0, -1, False, False), ('qQ', 6), ('qQ', 7), ('aQ', 3, 2, 4),
+    ('s2', 3, 0, 0, 1, -1, False, False), ('s2', 3, 0, 1, 1, -1, False, False), ('s1', 5, 1, 0, 2, 4), ('mu', 4, 0), ('mu', 4, 1),
+    ('s2', 2, 0, 0, 0, -1, False, False), ('s2', 2, 0, 1, 0, -1, False, False), ('s2', 3, 1, 0, 1, -1, False, True), ('s2', 3, 1, 1, 1, -1, False, True), ('mu', 4, 2),
+    ('mu', 4, 3), ('s2', 2, 1, 0, 0, -1, False, False), ('s2', 2, 1, 1, 0, -1, False, False), ('m', 0, 1), ('s1', 5, 2, 0, 2, 3),
+    ('aQ', 4, 0, 2), ('s2', 3, 0, 0, 0, -1, False, False), ('s2', 3, 0, 1, 0, -1, False, False), ('sg', 5, 0, 0), ('sg', 5, 0, 1),
+    ('sg', 5, 0, 2), ('sg', 5, 0, 3), ('sg', 5, 1, 0), ('sg', 5, 1, 1), ('sg', 5, 1, 2),
+    ('sg', 5, 1, 3), ('s2', 3, 1, 0, 0, -1, False, True), ('s2', 3, 1, 1, 0, -1, False, True), ('aQ', 4, 2, 4), ('m', 1, 1),
+    ('xb', 1, 5), ('m', 0, 0), ('s1', 5, 3, 0, 2, 2), ('s1', 6, 0, 0, 2, 4), ('s1', 6, 1, 0, 2, 5),
+    ('s1', 6, 2, 0, 2, 6), ('sg', 5, 2, 0), ('sg', 5, 2, 1), ('sg', 5, 2, 2), ('sg', 5, 2, 3),
+    ('s2', 4, 0, 0, 0, 3, True, False), ('s2', 4, 1, 0, 0, 3, False, False), ('sg', 5, 3, 0), ('sg', 5, 3, 1), ('sg', 5, 3, 2),
+    ('sg', 5, 3, 3), ('sg', 6, 0, 0), ('sg', 6, 0, 1), ('sg', 6, 0, 2), ('sg', 6, 0, 3),
+    ('m', 1, 0), ('s1', 6, 3, 0, 2, 0), ('mu', 5, 0), ('mu', 5, 1), ('mu', 5, 2),
+    ('mu', 5, 3), ('aQ', 5, 0, 2), ('s2', 4, 2, 0, 0, -1, False, False), ('s2', 4, 3, 0, 0, -1, False, False), ('aQ', 5, 2, 4),
+    ('xb', 2, 7), ('s2', 4, 0, 0, 1, 2, True, False), ('s2', 4, 1, 0, 1, 2, False, False), ('y', 0, 0, 2, 9), ('s1', 7, 0, 0, 2, 1),
+    ('s1', 7, 1, 0, 2, 4), ('s2', 4, 2, 0, 1, -1, False, False), ('s2', 4, 3, 0, 1, -1, False, False), ('sg', 6, 1, 0), ('sg', 6, 1, 1),
+    ('sg', 6, 1, 2), ('sg', 6, 1, 3), ('s1', 7, 2, 0, 2, 5), ('sg', 6, 2, 0), ('sg', 6, 2, 1),
+    ('sg', 6, 2, 2), ('sg', 6, 2, 3), ('s1', 7, 3, 0, 2, 6), ('s2', 5, 0, 0, 0, -1, False, False), ('s2', 5, 1, 0, 0, -1, False, False),
+    ('sg', 6, 3, 0), ('sg', 6, 3, 1), ('sg', 6, 3, 2), ('sg', 6, 3, 3), ('s2', 5, 2, 0, 0, -1, False, False),
+    ('s2', 5, 3, 0, 0, -1, False, True), ('y', 1, 0, 2, 11), ('mu', 6, 0), ('mu', 6, 1), ('mu', 6, 2),
+    ('mu', 6, 3), ('m', 2, 0), ('aQ', 6, 2, 4), ('sg', 7, 0, 0), ('sg', 7, 0, 1),
+    ('sg', 7, 0, 2), ('sg', 7, 0, 3), ('s2', 5, 0, 0, 1, -1, False, False), ('s2', 5, 1, 0, 1, -1, False, False), ('sg', 7, 1, 0),
+    ('sg', 7, 1, 1), ('sg', 7, 1, 2), ('sg', 7, 1, 3), ('sg', 7, 2, 0), ('sg', 7, 2, 1),
+    ('sg', 7, 2, 2), ('sg', 7, 2, 3), ('aQ', 6, 0, 2), ('sg', 7, 3, 0), ('sg', 7, 3, 1),
+    ('sg', 7, 3, 2), ('sg', 7, 3, 3), ('yR', 0, 1), ('yR', 1, 0), ('s2', 5, 2, 0, 1, -1, False, False),
+    ('s2', 5, 3, 0, 1, -1, False, True), ('m', 2, 1), ('s2', 6, 0, 0, 0, 0, True, False), ('s2', 6, 1, 0, 0, 0, False, False), ('mu', 7, 0),
+    ('mu', 7, 1), ('yR', 0, 0), ('mu', 7, 3), ('s2', 6, 0, 0, 1, 1, True, False), ('s2', 6, 1, 0, 1, 1, False, False),
+    ('yT', 0, 4), ('yR', 1, 1), ('mu', 7, 2), ('aQ', 7, 0, 2), ('yT', 1, 5),
+    ('aQ', 7, 2, 3), ('s2', 6, 2, 0, 1, -1, False, False), ('s2', 6, 3, 0, 1, -1, False, False), ('yC', 0, False), ('yQ', 0),
+    ('aQ', 7, 3, 4), ('s2', 6, 2, 0, 0, -1, False, False), ('s2', 6, 3, 0, 0, -1, False, False), ('s2', 7, 0, 0, 0, -1, False, False), ('s2', 7, 1, 0, 0, -1, False, False),
+    ('s2', 7, 2, 0, 0, -1, False, False), ('xb', 3, 12), ('yC', 1, False), ('s2', 7, 3, 0, 0, -1, False, True), ('y', 2, 0, 1, 292),
+    ('y', 2, 1, 2, 293), ('yR', 2, 0), ('s2', 7, 0, 0, 1, -1, False, False), ('s2', 7, 1, 0, 1, -1, False, False), ('m', 3, 0),
+    ('s2', 7, 2, 0, 1, -1, False, False), ('s2', 7, 3, 0, 1, -1, False, True), ('yQ', 1), ('yR', 2, 1), ('yT', 2, 6),
+    ('y', 3, 0, 1, 297), ('m', 3, 1), ('yT', 3, 3), ('yC', 2, False), ('yC', 3, False),
+    ('yR', 3, 0), ('yQ', 2), ('yD', 3, 1), ('yT', 4, 2), ('yC', 4, False),
+    ('yQ', 3), ('y', 3, 1, 2, 298), ('yT', 5, 4), ('yC', 5, True), ('yQ', 4),
     ('yQ', 5),
 ]
 
@@ -390,7 +390,7 @@ def tile_sigmoid_attention_folded_output_h1_kernel(
                 live["m", i] = work.tile([P, E], F32, name="m", bufs=4)
             cols = slice(eg * 512, (eg + 1) * 512)
             nc.vector.tensor_tensor(
-                out=live["m", i][:, cols], in0=live["acc", c, j, eg][:], in1=ls_rows[:, cols], op=ALU.mult)
+                out=live["m", i][:, cols], in0=ls_rows[:, cols], in1=live["acc", c, j, eg][:], op=ALU.mult)
 
         def finish_y(i, lo, hi, slot):
             y = shared(slot, [P, (hi - lo) * 512], F32)

from contextlib import ExitStack

import concourse.mybir as mybir
from concourse.masks import make_identity

H, T, D, S, E = 4, 512, 512, 1024, 1024
FLOPS = 2 * H * T * D * S + 2 * T * H * S * E

F32 = mybir.dt.float32
BF16 = mybir.dt.bfloat16
U32 = mybir.dt.uint32
I32 = mybir.dt.int32
U8 = mybir.dt.uint8
FP8X4 = mybir.dt.float8_e4m3fn_x4
FP4X4 = mybir.dt.float4_e2m1fn_x4
ACT = mybir.ActivationFunctionType
ALU = mybir.AluOpType

P = 128
RUN = 4
CHUNKS = [256, 128, 128]
SIG_BUFS = 4
GAIN_IN_PSUM = True
NEED_GAIN = False
Y_GROUPS = [[(0, 0), (1, 0)], [(0, 1), (1, 1)], [(2, 0)], [(2, 1)], [(3, 0)], [(3, 1)]]
LOADS = [('lq', 0), ('lktw', 0, 2), ('lq', 1), ('lkts', 0), ('lrows', 0), ('lqq', 1), ('lls',), ('lob',), ('lqq', 2), ('lvos', 0), ('lvo', 0, 0), ('lvo', 0, 1), ('lx', 0), ('lqq', 3), ('lvos', 1), ('lvo', 1, 0), ('lvo', 1, 1), ('lx', 1), ('lbc',)]
ORDER = [
    ('qT', 0, 0), ('pw', 0), ('qT', 1, 1), ('qC', 0, False), ('rT', 7),
    ('ps', 0), ('qQ', 0), ('s1', 0, 0, 0, 1, 2), ('s1', 0, 1, 0, 1, 3), ('s1', 0, 2, 0, 1, 4),
    ('qC', 1, False), ('rC',), ('s1', 0, 3, 0, 1, 5), ('qQ', 1), ('pw', 1),
    ('s1', 0, 0, 1, 2, 6), ('s1', 0, 1, 1, 2, 0), ('s1', 0, 2, 1, 2, 1), ('sg', 0, 0, 0), ('qT', 2, 2),
    ('sg', 0, 1, 0), ('sg', 0, 2, 0), ('sg', 0, 3, 0), ('col',), ('sg', 0, 0, 1),
    ('sg', 0, 1, 1), ('qT', 3, 3), ('s1', 0, 3, 1, 2, 4), ('sg', 0, 2, 1), ('ps', 1),
    ('mu', 0, 0), ('s1', 1, 0, 0, 2, 5), ('s1', 1, 1, 0, 2, 6), ('s1', 1, 2, 0, 2, 0), ('qC', 3, True),
    ('qC', 2, False), ('sg', 0, 3, 1), ('s1', 1, 3, 0, 2, 1), ('sg', 1, 0, 0), ('sg', 1, 0, 1),
    ('bT', 1, 0, 2), ('aQ', 0, 0, 2), ('qT', 4, 4), ('qQ', 3), ('qQ', 2),
    ('sg', 1, 1, 0), ('sg', 1, 1, 1), ('mu', 0, 1), ('sg', 1, 2, 0), ('sg', 1, 2, 1),
    ('sg', 1, 3, 0), ('sg', 1, 3, 1), ('s1', 2, 0, 0, 2, 3), ('s2', 0, 0, 0, 1, 5, True, False), ('s2', 0, 0, 1, 1, 6, True, False),
    ('s1', 2, 1, 0, 2, 0), ('qT', 5, 1), ('qC', 4, False), ('sg', 2, 0, 0), ('sg', 2, 0, 1),
    ('sg', 2, 1, 0), ('sg', 2, 1, 1), ('bC', 1, 0, True), ('bT', 1, 1, 2), ('mu', 1, 0),
    ('aQ', 0, 2, 4), ('mu', 1, 1), ('s1', 2, 2, 0, 2, 4), ('aQ', 1, 0, 2), ('qQ', 4),
    ('s1', 2, 3, 0, 2, 3), ('qC', 5, False), ('bC', 1, 1, False), ('qQ', 5), ('sg', 2, 2, 0),
    ('sg', 2, 2, 1), ('sg', 2, 3, 0), ('sg', 2, 3, 1), ('s2', 0, 1, 0, 1, -1, False, False), ('s2', 0, 1, 1, 1, -1, False, False),
    ('s1', 3, 0, 0, 2, 0), ('aQ', 1, 2, 4), ('s1', 3, 1, 0, 2, 1), ('qT', 6, 2), ('qT', 7, 4),
    ('qC', 6, False), ('s1', 3, 2, 0, 2, 3), ('s2', 1, 0, 0, 1, -1, False, False), ('s2', 1, 0, 1, 1, -1, False, False), ('mu', 2, 0),
    ('sg', 3, 0, 0), ('sg', 3, 0, 1), ('s1', 3, 3, 0, 2, 2), ('sg', 3, 1, 0), ('sg', 3, 1, 1),
    ('xb', 0, 3), ('sg', 3, 2, 0), ('sg', 3, 2, 1), ('s2', 1, 1, 0, 1, -1, False, False), ('s2', 1, 1, 1, 1, -1, False, False),
    ('s2', 0, 0, 0, 0, 0, True, False), ('s2', 0, 0, 1, 0, 1, True, False), ('mu', 2, 1), ('aQ', 2, 0, 2), ('aQ', 2, 2, 4),
    ('sg', 3, 3, 0), ('sg', 3, 3, 1), ('mu', 3, 1), ('s2', 0, 1, 0, 0, -1, False, False), ('s2', 0, 1, 1, 0, -1, False, False),
    ('mu', 3, 0), ('s1', 4, 0, 0, 2, 3), ('s2', 2, 0, 0, 1, -1, False, False), ('s2', 2, 0, 1, 1, -1, False, False), ('qC', 7, False),
    ('s1', 4, 1, 0, 2, 2), ('sg', 4, 0, 0), ('sg', 4, 0, 1), ('sg', 4, 0, 2), ('sg', 4, 0, 3),
    ('s1', 4, 2, 0, 2, 4), ('s2', 2, 1, 0, 1, -1, False, False), ('s2', 2, 1, 1, 1, -1, False, False), ('s1', 4, 3, 0, 2, 3), ('sg', 4, 1, 0),
    ('sg', 4, 1, 1), ('sg', 4, 1, 2), ('sg', 4, 1, 3), ('sg', 4, 2, 0), ('sg', 4, 2, 1),
    ('sg', 4, 2, 2), ('sg', 4, 2, 3), ('sg', 4, 3, 0), ('sg', 4, 3, 1), ('sg', 4, 3, 2),
    ('sg', 4, 3, 3), ('s2', 1, 0, 0, 0, -1, False, False), ('s2', 1, 0, 1, 0, -1, False, False), ('s1', 5, 0, 0, 2, 2), ('aQ', 3, 0, 2),
    ('s2', 1, 1, 0, 0, -1, False, False), ('s2', 1, 1, 1, 0, -1, False, False), ('qQ', 6), ('qQ', 7), ('aQ', 3, 2, 4),
    ('s2', 3, 0, 0, 1, -1, False, False), ('s2', 3, 0, 1, 1, -1, False, False), ('s1', 5, 1, 0, 2, 4), ('mu', 4, 0), ('mu', 4, 1),
    ('s2', 2, 0, 0, 0, -1, False, False), ('s2', 2, 0, 1, 0, -1, False, False), ('s2', 3, 1, 0, 1, -1, False, True), ('s2', 3, 1, 1, 1, -1, False, True), ('mu', 4, 2),
    ('mu', 4, 3), ('s2', 2, 1, 0, 0, -1, False, False), ('s2', 2, 1, 1, 0, -1, False, False), ('m', 0, 1), ('s1', 5, 2, 0, 2, 3),
    ('aQ', 4, 0, 2), ('s2', 3, 0, 0, 0, -1, False, False), ('s2', 3, 0, 1, 0, -1, False, False), ('sg', 5, 0, 0), ('sg', 5, 0, 1),
    ('sg', 5, 0, 2), ('sg', 5, 0, 3), ('sg', 5, 1, 0), ('sg', 5, 1, 1), ('sg', 5, 1, 2),
    ('sg', 5, 1, 3), ('s2', 3, 1, 0, 0, -1, False, True), ('s2', 3, 1, 1, 0, -1, False, True), ('aQ', 4, 2, 4), ('m', 1, 1),
    ('xb', 1, 5), ('m', 0, 0), ('s1', 5, 3, 0, 2, 2), ('s1', 6, 0, 0, 2, 4), ('s1', 6, 1, 0, 2, 5),
    ('s1', 6, 2, 0, 2, 6), ('sg', 5, 2, 0), ('sg', 5, 2, 1), ('sg', 5, 2, 2), ('sg', 5, 2, 3),
    ('s2', 4, 0, 0, 0, 3, True, False), ('s2', 4, 1, 0, 0, 3, False, False), ('sg', 5, 3, 0), ('sg', 5, 3, 1), ('sg', 5, 3, 2),
    ('sg', 5, 3, 3), ('sg', 6, 0, 0), ('sg', 6, 0, 1), ('sg', 6, 0, 2), ('sg', 6, 0, 3),
    ('m', 1, 0), ('s1', 6, 3, 0, 2, 0), ('mu', 5, 0), ('mu', 5, 1), ('mu', 5, 2),
    ('mu', 5, 3), ('aQ', 5, 0, 2), ('s2', 4, 2, 0, 0, -1, False, False), ('s2', 4, 3, 0, 0, -1, False, False), ('aQ', 5, 2, 4),
    ('xb', 2, 7), ('s2', 4, 0, 0, 1, 2, True, False), ('s2', 4, 1, 0, 1, 2, False, False), ('y', 0, 0, 2, 9), ('s1', 7, 0, 0, 2, 1),
    ('s1', 7, 1, 0, 2, 4), ('s2', 4, 2, 0, 1, -1, False, False), ('s2', 4, 3, 0, 1, -1, False, False), ('sg', 6, 1, 0), ('sg', 6, 1, 1),
    ('sg', 6, 1, 2), ('sg', 6, 1, 3), ('s1', 7, 2, 0, 2, 5), ('sg', 6, 2, 0), ('sg', 6, 2, 1),
    ('sg', 6, 2, 2), ('sg', 6, 2, 3), ('s1', 7, 3, 0, 2, 6), ('s2', 5, 0, 0, 0, -1, False, False), ('s2', 5, 1, 0, 0, -1, False, False),
    ('sg', 6, 3, 0), ('sg', 6, 3, 1), ('sg', 6, 3, 2), ('sg', 6, 3, 3), ('s2', 5, 2, 0, 0, -1, False, False),
    ('s2', 5, 3, 0, 0, -1, False, True), ('y', 1, 0, 2, 11), ('mu', 6, 0), ('mu', 6, 1), ('mu', 6, 2),
    ('mu', 6, 3), ('m', 2, 0), ('aQ', 6, 2, 4), ('sg', 7, 0, 0), ('sg', 7, 0, 1),
    ('sg', 7, 0, 2), ('sg', 7, 0, 3), ('s2', 5, 0, 0, 1, -1, False, False), ('s2', 5, 1, 0, 1, -1, False, False), ('sg', 7, 1, 0),
    ('sg', 7, 1, 1), ('sg', 7, 1, 2), ('sg', 7, 1, 3), ('sg', 7, 2, 0), ('sg', 7, 2, 1),
    ('sg', 7, 2, 2), ('sg', 7, 2, 3), ('aQ', 6, 0, 2), ('sg', 7, 3, 0), ('sg', 7, 3, 1),
    ('sg', 7, 3, 2), ('sg', 7, 3, 3), ('yR', 0, 1), ('yR', 1, 0), ('s2', 5, 2, 0, 1, -1, False, False),
    ('s2', 5, 3, 0, 1, -1, False, True), ('m', 2, 1), ('s2', 6, 0, 0, 0, 0, True, False), ('s2', 6, 1, 0, 0, 0, False, False), ('mu', 7, 0),
    ('mu', 7, 1), ('yR', 0, 0), ('mu', 7, 3), ('s2', 6, 0, 0, 1, 1, True, False), ('s2', 6, 1, 0, 1, 1, False, False),
    ('yT', 0, 4), ('yR', 1, 1), ('mu', 7, 2), ('aQ', 7, 0, 2), ('yT', 1, 5),
    ('aQ', 7, 2, 3), ('s2', 6, 2, 0, 1, -1, False, False), ('s2', 6, 3, 0, 1, -1, False, False), ('yC', 0, False), ('yQ', 0),
    ('aQ', 7, 3, 4), ('s2', 6, 2, 0, 0, -1, False, False), ('s2', 6, 3, 0, 0, -1, False, False), ('s2', 7, 0, 0, 0, -1, False, False), ('s2', 7, 1, 0, 0, -1, False, False),
    ('s2', 7, 2, 0, 0, -1, False, False), ('xb', 3, 12), ('yC', 1, False), ('s2', 7, 3, 0, 0, -1, False, True), ('y', 2, 0, 1, 292),
    ('y', 2, 1, 2, 293), ('yR', 2, 0), ('s2', 7, 0, 0, 1, -1, False, False), ('s2', 7, 1, 0, 1, -1, False, False), ('m', 3, 0),
    ('s2', 7, 2, 0, 1, -1, False, False), ('s2', 7, 3, 0, 1, -1, False, True), ('yQ', 1), ('yR', 2, 1), ('yT', 2, 6),
    ('y', 3, 0, 1, 297), ('m', 3, 1), ('yT', 3, 3), ('yC', 2, False), ('yC', 3, False),
    ('yR', 3, 0), ('yQ', 2), ('yD', 3, 1), ('yT', 4, 2), ('yC', 4, False),
    ('yQ', 3), ('y', 3, 1, 2, 298), ('yT', 5, 4), ('yC', 5, True), ('yQ', 4),
    ('yQ', 5),
]


def tile_sigmoid_attention_folded_output_h1_kernel(
    tc, queries, kt_words, kt_scales, score_bias, key_gain, vo_words, vo_scales,
    out_bias, layer_scale, x, out_0, out_1, out_2,
):
    nc = tc.nc
    starts = [sum(CHUNKS[:c]) for c in range(len(CHUNKS))]
    units = []
    for c, n in enumerate(CHUNKS):
        for hg in range(H * n // 512):
            for g in range(2):
                units.append((c, hg, g))
    tiles = [(c, j) for c, n in enumerate(CHUNKS) for j in range(n // P)]

    with ExitStack() as ctx:
        keep = ctx.enter_context(tc.tile_pool(name="keep", bufs=1))
        work = ctx.enter_context(tc.tile_pool(name="work", bufs=2))
        psum = ctx.enter_context(tc.psum_pool(name="psum", bufs=1))
        ctx.enter_context(tc.manual_schedule())

        def kept(name, shape, dtype):
            return keep.tile(shape, dtype, name=name, align_bytes=64)

        warm_in = kept("warm_in", [P, 8], F32)
        warm_out = kept("warm_out", [P, 8], F32)
        ident_f32 = kept("ident_f32", [P, P], F32)
        ktw_raw = kept("ktw_raw", [P, 2 * S], U8)
        kts_raw = kept("kts_raw", [P, S], U8)
        ktw = kept("ktw", [P, 2 * S], U8)
        kts = kept("kts", [P, S], U8)
        key_rows = kept("key_rows", [P, 512], BF16)
        bias = kept("bias", [P, 8, 4], F32)
        gain = kept("gain", [P, 8, 4 * RUN], F32)
        vos = kept("vos", [P, 8, E], U8)
        vow = {(hp, g): kept("vow%d%d" % (hp, g), [P, 2, 2 * E], U8) for hp in range(2) for g in range(2)}
        q_pair = {b: kept("q_raw%d" % b, [P, 2, 2, D], BF16) for b in range(4)}
        q_raw = {b: q_pair[b // 2][:, b % 2] for b in range(8)}
        q_codes = {b: kept("q_codes%d" % b, [P, 512], U32) for b in range(4)}
        q_scales = {b: kept("q_scales%d" % b, [P, 512], U8) for b in range(4)}
        ls_col = kept("ls_col", [P, 8], BF16)
        ob_col = kept("ob_col", [P, 8], BF16)
        cols32 = kept("cols32", [P, 2, 8], F32)
        ls_rows = kept("ls_rows", [P, E], BF16)
        ob_rows = kept("ob_rows", [P, E], BF16)
        rows32 = [ls_rows, kept("lsb_rows", [P, E], F32)]
        live = {"lsb": rows32[1]}
        x_sb = {i: kept("x_sb%d" % i, [P, 2, E], BF16) for i in range(2)}
        y_codes = kept("y_codes", [P, 2, T], U32)
        y_scales = kept("y_scales", [P, 2, T], U8)

        def bank_tile(b, shape, dtype):
            return psum.tile(shape, dtype, name="bank", tag="bank%d" % b)

        def shared(slot, shape, dtype):
            return keep.tile(shape, dtype, name="shared", tag="slot%d" % slot, align_bytes=64)

        def q_block(b):
            k = 2 * (b // 2)
            c, hg, g = units[k]
            return c, hg, b % 2

        def load_q(b):
            c, hg, half = q_block(b)
            rows = slice(starts[c], starts[c] + CHUNKS[c])
            if CHUNKS[c] == 256:
                src = queries[2 * hg + half, rows, :].rearrange("(p n) d -> p n d", n=2)
            else:
                src = queries[2 * half:2 * half + 2, rows, :].rearrange("n p d -> p n d")
            nc.sync.dma_start(out=q_raw[b], in_=src)

        def load_q_pair(b):
            c, hg, half = q_block(2 * b)
            rows = slice(starts[c], starts[c] + CHUNKS[c])
            if CHUNKS[c] == 256:
                src = queries[2 * hg:2 * hg + 2, rows, :].rearrange("h (p n) d -> p h (n d)", n=2)
                dst = q_pair[b][:].rearrange("p h n d -> p h (n d)")
            else:
                src = queries[:, rows, :].rearrange("h p d -> p h d")
                dst = q_pair[b][:].rearrange("p h n d -> p (h n) d")
            nc.sync.dma_start(out=dst, in_=src)

        def load_vo(hp, g):
            nc.sync.dma_start(
                out=vow[hp, g][:].bitcast(I32),
                in_=vo_words[4 * hp + g:4 * hp + 4:2].rearrange("k p n -> p k n").bitcast(I32))

        def load_x(i):
            nc.sync.dma_start(
                out=x_sb[i][:], in_=x[i * 256:(i + 1) * 256, :].rearrange("(j p) e -> p j e", j=2))

        def load_ktw(lo, hi):
            cols = slice(lo * 1024, hi * 1024)
            nc.sync.dma_start(out=ktw_raw[:, cols].bitcast(I32), in_=kt_words[0, :, cols].bitcast(I32))

        def load_kts(on_scalar):
            queue = nc.scalar if on_scalar else nc.sync
            for quad in range(4):
                queue.dma_start(
                    out=kts_raw[32 * quad:32 * quad + 4, :].bitcast(I32),
                    in_=kt_scales[0, 4 * quad:4 * quad + 4, :].bitcast(I32))

        def load_rows(on_scalar):
            queue = nc.scalar if on_scalar else nc.sync
            queue.dma_start(out=key_rows[0:8, :], in_=score_bias.rearrange("h (g k) -> (h g) k", g=2))
            queue.dma_start(out=key_rows[8:16, :], in_=key_gain.rearrange("h (g k) -> (h g) k", g=2))

        def load_vos(hp):
            for quad in range(4):
                nc.sync.dma_start(
                    out=vos[32 * quad:32 * quad + 4, 4 * hp:4 * hp + 4, :].bitcast(I32),
                    in_=vo_scales[4 * hp:4 * hp + 4, 4 * quad:4 * quad + 4, :].rearrange("k r n -> r k n").bitcast(I32))

        def load_ls():
            nc.sync.dma_start(out=ls_col[:], in_=layer_scale.rearrange("(p c) -> p c", c=8))

        def load_ls_rows():
            nc.sync.dma_start(out=ls_rows[:], in_=layer_scale.partition_broadcast(P))

        def load_ob_rows():
            nc.sync.dma_start(out=ob_rows[:], in_=out_bias.partition_broadcast(P))

        def load_ob():
            nc.sync.dma_start(out=ob_col[:], in_=out_bias.rearrange("(p c) -> p c", c=8))

        def permute_kt_words(g):
            cols = slice(g * 1024, (g + 1) * 1024)
            nc.vector.tensor_copy(
                out=ktw[:, cols].rearrange("p (t m b) -> p t m b", t=4, b=2),
                in_=ktw_raw[:, cols].rearrange("p (m t b) -> p t m b", t=4, b=2))

        def permute_kt_scales(g):
            cols = slice(g * 512, (g + 1) * 512)
            nc.vector.tensor_copy(
                out=kts[:, cols].rearrange("p (t m) -> p t m", t=4),
                in_=kts_raw[:, cols].rearrange("p (m t) -> p t m", t=4))

        def turn_key_rows(bk):
            bank = bank_tile(bk, [P, 2 * P], F32)
            words = key_rows[:].bitcast(F32)
            for u in range(2):
                nc.tensor.transpose(bank[:, u:2 * P:2], words[:, u:256:2], ident_f32[:])
            live["rows"] = bank[:].bitcast(BF16).rearrange("p (r t) -> p r t", t=4)

        def take_key_rows():
            bank = live["rows"]
            nc.vector.tensor_copy(out=bias[:], in_=bank[:, 0:8, :])
            if NEED_GAIN:
                nc.vector.tensor_copy(
                    out=gain[:].rearrange("p r (t i) -> p r t i", i=RUN),
                    in_=bank[:, 8:16, :].unsqueeze(3).to_broadcast([P, 8, 4, RUN]))

        def turn_q(b, bk):
            bank = bank_tile(bk, [P, 4, P], F32)
            words = q_raw[b].bitcast(F32)
            for n in range(2):
                for u in range(2):
                    nc.tensor.transpose(bank[:, 2 * n + u, :], words[:, n, u:256:2], ident_f32[:])
            live["qbank", b] = bank

        def copy_q(b, on_vector):
            grouped = work.tile([P, 1024], BF16, name="q_grouped", bufs=4, align_bytes=64)
            if CHUNKS[q_block(b)[0]] == 256:
                dst = grouped[:].bitcast(F32).rearrange("p (r w) -> p r w", w=4)
                src = live["qbank", b][:].rearrange("p w r -> p r w")
            else:
                dst = grouped[:].bitcast(F32).rearrange("p (n r u) -> p n r u", n=2, u=2)
                src = live["qbank", b][:].rearrange("p (n u) r -> p n r u", n=2)
            if on_vector:
                nc.vector.tensor_copy(out=dst, in_=src)
            else:
                nc.scalar.copy(out=dst, in_=src)
            live["qg", b] = grouped

        def quant_q(b):
            cols = slice((b % 2) * 256, (b % 2 + 1) * 256)
            nc.vector.quantize_mx(
                out=q_codes[b // 2][:, cols].bitcast(FP8X4), scales=q_scales[b // 2][:, cols], in_=live["qg", b][:])

        def pass_of(k, hh):
            c, hg, g = units[k]
            return 2 * (hg * 512 // CHUNKS[c] + hh) + g

        def scores(k, t, lo, hi, bk):
            c, hg, g = units[k]
            bank = bank_tile(bk, [P, 512], F32)
            slot = 4 * g + t
            cols = slice(lo * 256, hi * 256)
            nc.tensor.matmul_mx(
                out=bank[:, cols],
                lhsT=ktw[:, slot * 256:(slot + 1) * 256].bitcast(FP4X4),
                lhsT_scale=kts[:, slot * 128:(slot + 1) * 128],
                rhs=q_codes[k // 2][:, cols].bitcast(FP8X4),
                rhs_scale=q_scales[k // 2][:, cols],
                start=True, stop=True)
            for half in range(lo, hi):
                live["s", k, t, half] = bank

        def sigmoid(k, t, hh):
            n = CHUNKS[units[k][0]]
            if ("sig", k) not in live:
                live["sig", k] = work.tile([P, 512 // n, 4, n], F32, name="sig", bufs=SIG_BUFS)
            nc.scalar.activation(
                out=live["sig", k][:, hh, t, :], in_=live["s", k, t, hh * n // 256][:, hh * n:(hh + 1) * n],
                func=ACT.Sigmoid, bias=bias[:, pass_of(k, hh), t:t + 1])

        def a_cols(k, lo, hi):
            half = lo // 1024
            if ("a", k, half) not in live:
                live["a", k, half] = shared(2 * k + half, [P, 1024], BF16)
            return live["a", k, half][:, lo - half * 1024:hi - half * 1024]

        def apply_gain(k, hh):
            n = CHUNKS[units[k][0]]
            row = pass_of(k, hh)
            if GAIN_IN_PSUM:
                gains = live["rows"][:, 8 + row, :].unsqueeze(1).unsqueeze(3)
            else:
                gains = gain[:, row, :].rearrange("p (t i) -> p t i", i=RUN).unsqueeze(1)
            nc.vector.tensor_tensor(
                out=a_cols(k, hh * 4 * n, (hh + 1) * 4 * n).rearrange("p (c i t) -> p c t i", i=RUN, t=4),
                in0=live["sig", k][:, hh].rearrange("p t (c i) -> p c t i", i=RUN),
                in1=gains.to_broadcast([P, n // RUN, 4, RUN]),
                op=ALU.mult)

        def gain_rows(k, hh, t):
            n = CHUNKS[units[k][0]]
            if ("ar", k, hh) not in live:
                live["ar", k, hh] = work.tile([P, 4, n], BF16, name="a_rows", bufs=2, align_bytes=64)
            nc.scalar.activation(
                out=live["ar", k, hh][:, t, :], in_=live["sig", k][:, hh, t, :], func=ACT.Copy,
                scale=gain[:, pass_of(k, hh), RUN * t:RUN * t + 1])

        def interleave(k, hh):
            n = CHUNKS[units[k][0]]
            nc.vector.tensor_copy(
                out=a_cols(k, hh * 4 * n, (hh + 1) * 4 * n).rearrange("p (c i t) -> p c t i", i=4, t=4),
                in_=live["ar", k, hh][:].rearrange("p t (c i) -> p c t i", i=4))

        def quant_a(k, lo, hi):
            if ("aq", k) not in live:
                codes = work.tile([P, 512], U32, name="a_codes", bufs=4, align_bytes=64)
                scales = work.tile([P, 512], U8, name="a_scales", bufs=4, align_bytes=64)
                live["aq", k] = (codes, scales)
            codes, scales = live["aq", k]
            nc.vector.quantize_mx(
                out=codes[:, lo * P:hi * P].bitcast(FP8X4), scales=scales[:, lo * P:hi * P],
                in_=a_cols(k, lo * 512, hi * 512))

        def project(k, hh, j, eg, bk, first, last):
            c, hg, g = units[k]
            codes, scales = live["aq", k]
            row = pass_of(k, hh)
            if first:
                live["acc", c, j, eg] = bank_tile(bk, [P, 512], F32)
            cols = slice(hh * CHUNKS[c] + j * P, hh * CHUNKS[c] + (j + 1) * P)
            nc.tensor.matmul_mx(
                out=live["acc", c, j, eg][:],
                lhsT=codes[:, cols].bitcast(FP8X4),
                lhsT_scale=scales[:, cols],
                rhs=vow[row // 4, g][:, (row // 2) % 2, eg * 1024:(eg + 1) * 1024].bitcast(FP4X4),
                rhs_scale=vos[:, row, eg * 512:(eg + 1) * 512],
                start=first, stop=last)

        def engine(slot):
            return nc.vector if slot >= 100 else nc.gpsimd

        def make_lsb(slot):
            live["lsb"] = shared(slot, [P, E], F32)
            engine(slot).tensor_tensor(out=live["lsb"][:], in0=ls_rows[:], in1=ob_rows[:], op=ALU.mult)

        def make_cols():
            nc.vector.tensor_tensor(out=cols32[:, 1, :], in0=ls_col[:], in1=ob_col[:], op=ALU.mult)

        def spread(v, half, bk):
            bank = bank_tile(bk, [P, 4, P], F32)
            for c in range(4):
                col = cols32[:, v, 4 * half + c:4 * half + c + 1]
                nc.tensor.transpose(bank[:, c, :], col.to_broadcast([P, P]), ident_f32[:])
            live["spread", v, half] = bank

        def copy_spread(v, half, on_vector):
            dst = rows32[v][:].rearrange("p (q c) -> p q c", c=8)[:, :, 4 * half:4 * half + 4]
            src = live["spread", v, half][:].rearrange("p c q -> p q c")
            if on_vector:
                nc.vector.tensor_copy(out=dst, in_=src)
            else:
                nc.scalar.copy(out=dst, in_=src)

        def make_xb(i, slot):
            live["xb", i] = shared(slot, [P, E], F32)
            engine(slot).tensor_tensor(
                out=live["xb", i][:], in0=x_sb[i // 2][:, i % 2, :], in1=live["lsb"][:], op=ALU.add)

        def scale_o(i, eg):
            c, j = tiles[i]
            if ("m", i) not in live:
                live["m", i] = work.tile([P, E], F32, name="m", bufs=4)
            cols = slice(eg * 512, (eg + 1) * 512)
            nc.vector.tensor_tensor(
                out=live["m", i][:, cols], in0=ls_rows[:, cols], in1=live["acc", c, j, eg][:], op=ALU.mult)

        def finish_y(i, lo, hi, slot):
            y = shared(slot, [P, (hi - lo) * 512], F32)
            for eg in range(lo, hi):
                live["y", i, eg] = y[:, (eg - lo) * 512:(eg - lo + 1) * 512]
            cols = slice(lo * 512, hi * 512)
            engine(slot).tensor_tensor(
                out=y[:], in0=live["m", i][:, cols], in1=live["xb", i][:, cols], op=ALU.add)
            nc.sync.dma_start(out=out_0[i * P:(i + 1) * P, cols], in_=y[:])

        def round_y(i, eg):
            y16 = work.tile([P, 512], BF16, name="y16", bufs=4, align_bytes=64)
            nc.scalar.copy(
                out=y16[:].rearrange("p (u q i) -> p u q i", u=2, i=2),
                in_=live["y", i, eg].rearrange("p (q u i) -> p u q i", u=2, i=2))
            live["y16", i, eg] = y16

        def round_y_direct(i, eg):
            y16 = work.tile([P, 512], BF16, name="y16", bufs=4, align_bytes=64)
            cols = slice(eg * 512, (eg + 1) * 512)
            nc.vector.tensor_tensor(
                out=y16[:].rearrange("p (u q i) -> p u q i", u=2, i=2),
                in0=live["m", i][:, cols].rearrange("p (q u i) -> p u q i", u=2, i=2),
                in1=live["xb", i][:, cols].rearrange("p (q u i) -> p u q i", u=2, i=2), op=ALU.add)
            live["y16", i, eg] = y16

        def turn_y(grp, bk):
            pieces = Y_GROUPS[grp]
            bank = bank_tile(bk, [P, 2 * len(pieces), P], F32)
            for s, (i, eg) in enumerate(pieces):
                words = live["y16", i, eg][:].bitcast(F32)
                for u in range(2):
                    nc.tensor.transpose(bank[:, 2 * s + u, :], words[:, u * P:(u + 1) * P], ident_f32[:])
            live["ybank", grp] = bank

        def copy_y(grp, on_vector):
            pieces = Y_GROUPS[grp]
            grouped = work.tile([P, 512 * len(pieces)], BF16, name="y_grouped", bufs=2, align_bytes=64)
            dst = grouped[:].bitcast(F32).rearrange("p (s r u) -> p s r u", r=P, u=2)
            src = live["ybank", grp][:].rearrange("p (s u) r -> p s r u", u=2)
            if on_vector:
                nc.vector.tensor_copy(out=dst, in_=src)
            else:
                nc.scalar.copy(out=dst, in_=src)
            live["yg", grp] = grouped

        def quant_y(grp):
            pieces = Y_GROUPS[grp]
            i, eg = pieces[0]
            cols = slice(i * P, (i + len(pieces)) * P)
            nc.vector.quantize_mx(
                out=y_codes[:, eg, cols].bitcast(FP8X4), scales=y_scales[:, eg, cols], in_=live["yg", grp][:])
            nc.sync.dma_start(
                out=out_1[eg].rearrange("p m t -> p (m t)")[:, 4 * cols.start:4 * cols.stop].bitcast(I32),
                in_=y_codes[:, eg, cols].bitcast(I32))

        def store_y_scales():
            for quad in range(4):
                queue = nc.sync if quad % 2 == 0 else nc.scalar
                queue.dma_start(
                    out=out_2[:, 4 * quad:4 * quad + 4, :].rearrange("g r m -> r g m").bitcast(I32),
                    in_=y_scales[32 * quad:32 * quad + 4, :, :].bitcast(I32))

        steps = {
            "lq": load_q, "lqq": load_q_pair, "lbo": load_ob_rows, "lsb": make_lsb, "lvo": load_vo, "lx": load_x, "lktw": load_ktw, "lkts": load_kts, "lrows": load_rows,
            "lvos": load_vos, "lls": load_ls, "lob": load_ob, "lbc": load_ls_rows,
            "pw": permute_kt_words, "ps": permute_kt_scales, "rT": turn_key_rows, "rC": take_key_rows,
            "qT": turn_q, "qC": copy_q, "qQ": quant_q, "s1": scores, "sg": sigmoid, "mu": apply_gain,
            "aQ": quant_a, "ga": gain_rows, "il": interleave, "s2": project, "col": make_cols, "bT": spread, "bC": copy_spread, "yD": round_y_direct, "xb": make_xb, "m": scale_o, "y": finish_y,
            "yR": round_y, "yT": turn_y, "yC": copy_y, "yQ": quant_y,
        }

        nc.vector.memset(kts_raw[:].bitcast(I32), 0)
        nc.vector.memset(key_rows[:], 0.0)
        nc.vector.memset(warm_in[:], 0.0)
        nc.vector.memset(vos[:].rearrange("p k n -> p (k n)").bitcast(I32), 0)
        make_identity(nc, ident_f32[:])
        for step in LOADS:
            steps[step[0]](*step[1:])
        nc.scalar.activation(out=warm_out[:], in_=warm_in[:], func=ACT.Sigmoid)
        for step in ORDER:
            steps[step[0]](*step[1:])
        store_y_scales()
